import numpy as np
CORES = [96,97,98,99,224,225,226,227,352,353,354,355,480,481,482,483]
N = 16
T = 512
ROUTE = [[[14,9,4],[14,15,5],[14,0,1],[14,5,4],[10,14,2],[14,2,5],[0,2,5],[14,3,15],[14,11,10],[8,10,5],[14,4,5],[1,14,0],[14,0,5],[12,9,14],[14,5,0],[14,1,9],[14,5,6],[4,14,5],[14,0,6],[14,0,12],[11,14,7],[11,14,15],[0,5,14],[14,13,3],[4,7,10],[9,4,14],[14,10,3],[14,13,1],[8,2,10],[14,4,5],[14,4,11],[6,11,14],[14,1,13],[1,14,3],[14,9,0],[10,15,14],[2,4,3],[14,4,8],[14,4,9],[9,0,14],[14,7,11],[1,15,14],[0,14,13],[11,8,6],[10,14,4],[15,12,11],[14,8,15],[13,2,14],[2,14,13],[8,14,11],[13,9,10],[14,4,5],[14,9,15],[14,8,2],[14,13,8],[0,12,14],[8,12,3],[9,14,4],[11,0,13],[0,13,14],[8,14,3],[14,4,2],[14,12,15],[1,0,14],[1,14,13],[4,6,14],[2,14,3],[14,15,7],[7,14,3],[9,14,11],[9,14,15],[14,15,3],[7,14,13],[14,9,0],[5,4,14],[3,14,15],[11,14,6],[5,14,10],[6,13,14],[13,8,14],[8,14,3],[10,14,12],[14,15,6],[4,8,2],[15,14,1],[14,10,7],[11,14,1],[14,6,8],[4,12,14],[14,2,5],[15,14,0],[10,13,5],[9,14,4],[14,0,5],[14,1,15],[3,13,1],[14,0,7],[14,5,11],[3,14,13],[14,1,15],[14,9,4],[14,11,2],[14,12,3],[14,1,13],[10,3,2],[14,4,6],[8,6,15],[14,8,13],[2,13,15],[15,14,4],[12,3,4],[9,14,15],[12,5,14],[5,14,2],[14,15,9],[13,14,15],[14,3,6],[3,14,15],[7,10,13],[2,14,3],[12,14,13],[0,12,14],[14,13,0],[7,2,14],[14,12,15],[14,4,12],[6,0,14],[14,12,0],[0,10,7],[14,1,15],[15,14,11],[14,15,3],[1,14,0],[4,15,7],[14,7,0],[2,14,11],[14,1,2],[0,14,11],[14,2,7],[14,3,2],[13,4,12],[14,11,13],[13,6,14],[14,11,10],[14,9,10],[14,15,11],[1,14,8],[13,2,4],[14,4,0],[14,3,0],[4,14,2],[14,8,11],[14,12,1],[14,1,3],[14,13,3],[11,3,5],[14,11,15],[14,10,2],[11,3,12],[14,9,7],[14,0,12],[14,13,9],[6,10,14],[10,14,8],[14,4,11],[4,14,12],[7,9,14],[1,11,14],[14,11,4],[12,8,3],[3,14,12],[14,15,4],[13,12,9],[14,10,11],[11,14,12],[14,4,12],[14,12,5],[5,14,0],[8,13,14],[5,6,12],[14,3,11],[14,11,1],[14,15,10],[4,14,11],[5,8,13],[14,9,10],[14,6,8],[5,14,7],[3,4,14],[14,12,10],[0,3,1],[10,9,14],[14,2,10],[14,2,3],[4,14,0],[14,1,8],[3,14,9],[14,9,0],[14,0,11],[14,0,10],[14,3,6],[14,11,10],[14,5,0],[14,6,8],[1,14,6],[3,6,10],[11,1,14],[7,10,6],[4,14,8],[14,12,1],[14,4,10],[14,7,0],[14,8,15],[7,14,15],[11,14,3],[14,0,4],[14,5,10],[14,0,1],[11,15,8],[14,10,0],[0,11,14],[9,1,4],[14,0,11],[1,14,5],[15,9,14],[12,14,8],[15,14,3],[8,4,14],[9,13,6],[10,8,14],[13,15,8],[6,14,0],[14,3,1],[7,1,10],[9,14,4],[14,2,8],[14,6,11],[2,5,15],[4,14,10],[14,13,11],[0,14,6],[14,7,4],[14,6,15],[11,14,2],[14,12,6],[8,14,0],[5,14,11],[15,14,12],[14,4,8],[0,4,12],[8,3,14],[2,3,14],[9,4,5],[4,14,9],[14,12,6],[14,6,9],[14,5,1],[14,8,0],[15,13,2],[3,7,9],[13,14,11],[1,14,9],[0,14,13],[14,11,1],[14,9,12],[0,14,8],[6,10,14],[14,11,5],[14,10,5],[14,8,6],[7,14,4],[0,5,3],[14,13,10],[3,14,9],[13,8,14],[15,14,0],[14,4,5],[14,9,6],[15,14,5],[14,10,8],[14,0,10],[14,9,11],[3,7,10],[14,13,8],[1,14,6],[14,3,8],[1,14,0],[14,0,5],[14,1,15],[4,1,3],[2,14,3],[14,7,11],[14,10,5],[4,8,12],[1,3,15],[14,11,7],[14,1,12],[14,6,9],[3,14,12],[14,7,1],[14,5,8],[8,14,10],[2,4,14],[2,14,9],[14,6,15],[14,1,4],[14,11,9],[0,5,14],[14,6,11],[14,7,2],[14,6,5],[10,14,0],[8,14,5],[14,2,6],[2,0,5],[14,7,4],[11,14,13],[14,5,9],[6,14,15],[14,13,5],[14,15,9],[14,10,13],[5,2,4],[14,15,10],[14,1,5],[2,6,14],[14,10,0],[14,9,10],[12,11,1],[15,8,14],[14,3,4],[10,12,14],[4,8,14],[14,12,8],[9,14,7],[2,13,0],[10,0,14],[6,11,2],[9,14,12],[14,12,7],[11,14,12],[14,1,0],[14,10,1],[12,10,14],[10,15,12],[14,13,11],[1,14,2],[2,14,8],[7,14,1],[14,13,10],[8,14,3],[4,11,14],[0,14,12],[12,10,3],[14,8,11],[8,14,12],[4,2,14],[4,6,5],[14,6,5],[12,7,14],[13,4,15],[1,12,13],[10,7,14],[11,1,14],[14,0,1],[14,0,15],[13,14,8],[0,12,14],[7,1,13],[14,5,2],[14,7,2],[7,4,8],[13,14,0],[12,14,11],[10,14,15],[14,8,15],[7,14,5],[0,5,1],[14,4,12],[14,0,9],[14,0,11],[11,5,1],[8,14,9],[15,5,2],[3,9,11],[8,1,9],[3,4,0],[5,14,3],[15,14,8],[2,8,11],[1,14,5],[14,12,5],[14,10,8],[14,4,2],[7,14,10],[0,14,6],[8,14,15],[10,14,6],[6,0,9],[15,13,1],[11,14,7],[14,9,12],[8,7,14],[11,14,15],[14,0,12],[14,12,4],[14,7,4],[14,1,13],[4,7,15],[14,13,4],[14,3,2],[11,6,14],[14,12,0],[14,11,1],[11,13,0],[4,11,7],[14,4,11],[14,1,8],[11,5,0],[8,4,2],[14,0,8],[14,13,12],[14,1,0],[14,12,2],[11,1,14],[4,14,0],[14,6,8],[14,4,9],[9,14,7],[1,9,5],[5,14,1],[9,14,8],[15,0,14],[7,0,9],[14,8,6],[14,6,3],[14,15,8],[11,14,6],[14,1,9],[14,9,11],[14,5,3],[0,3,8],[4,14,3],[12,9,14],[14,4,11],[1,7,14],[14,1,3],[13,14,0],[14,10,9],[14,0,1],[5,14,1],[8,14,9],[11,14,12],[14,15,4],[14,15,3],[14,0,7],[14,3,2],[3,2,14],[12,14,15],[5,14,6],[15,8,7],[14,11,9],[14,4,11],[12,8,1],[14,10,4],[14,5,2],[10,14,6],[2,14,1],[14,13,9],[14,7,15],[12,11,14],[3,5,14],[14,12,5],[14,2,4],[14,5,9],[14,7,0],[15,1,14],[14,12,4],[14,12,6],[7,15,2],[15,8,9],[13,14,15],[14,10,1],[14,4,11],[0,14,10],[8,14,2],[4,7,12],[0,10,2],[14,8,13],[8,5,14],[11,4,14],[14,7,2],[14,6,9],[14,8,6],[14,7,11],[0,7,14],[14,1,3],[14,13,2],[8,14,5],[1,0,14],[3,6,14],[9,14,7],[9,14,6],[6,4,14],[14,10,3],[0,3,14],[0,8,14],[9,11,14],[14,1,7],[7,14,9],[14,3,10],[14,15,10]],[[14,15,6],[14,4,9],[14,6,15],[14,15,2],[5,9,7],[14,11,9],[15,14,4],[14,11,13],[14,10,15],[12,14,11],[14,12,5],[14,3,0],[14,0,5],[14,1,15],[14,15,2],[14,12,10],[1,14,4],[11,0,14],[5,12,14],[14,11,3],[14,15,4],[0,10,14],[14,7,10],[2,5,3],[12,1,3],[14,15,5],[9,14,4],[14,6,4],[14,8,12],[14,6,8],[14,8,5],[5,14,8],[14,0,3],[14,1,11],[1,0,15],[1,4,11],[15,10,14],[14,10,4],[14,5,9],[6,12,14],[7,14,12],[4,3,12],[11,5,9],[14,0,10],[3,14,13],[2,9,14],[14,4,15],[14,9,8],[15,1,9],[13,11,14],[6,14,0],[14,8,7],[8,12,14],[4,0,14],[11,5,10],[9,12,5],[14,5,10],[14,15,3],[7,10,14],[7,14,11],[14,12,10],[14,12,1],[10,14,1],[6,5,10],[14,6,4],[10,1,14],[14,2,0],[8,2,14],[14,12,4],[14,2,15],[14,6,12],[8,14,1],[14,5,9],[14,11,2],[14,7,11],[13,6,14],[4,2,14],[0,15,14],[15,14,6],[10,14,4],[12,11,14],[4,8,14],[9,4,13],[14,8,7],[11,14,1],[14,4,1],[14,13,12],[14,13,8],[14,9,7],[14,15,0],[14,11,5],[14,2,7],[14,15,13],[12,14,4],[14,11,4],[12,4,14],[14,5,12],[11,14,13],[13,14,0],[6,5,1],[2,9,8],[4,14,1],[10,2,14],[8,14,4],[12,4,14],[14,15,8],[14,11,4],[6,10,14],[6,14,2],[14,4,10],[10,15,6],[3,13,10],[14,7,6],[14,13,15],[14,12,15],[14,15,8],[11,15,5],[14,10,8],[14,7,0],[7,2,14],[14,15,8],[14,8,12],[14,15,1],[14,15,4],[14,1,5],[9,14,7],[11,5,14],[9,15,10],[4,14,11],[3,14,10],[15,12,9],[6,7,5],[14,12,10],[14,2,5],[14,0,3],[14,3,8],[14,13,6],[14,9,8],[7,13,14],[3,2,14],[1,12,14],[14,9,8],[13,11,14],[2,9,3],[14,9,8],[14,6,0],[15,14,6],[3,15,11],[11,12,14],[7,13,11],[14,8,1],[10,14,9],[2,14,13],[12,11,4],[14,6,10],[14,5,6],[14,7,9],[8,6,14],[4,14,10],[14,8,15],[14,0,8],[15,3,14],[6,4,14],[14,8,2],[4,6,14],[14,3,10],[11,14,2],[6,12,14],[3,9,14],[2,14,7],[14,5,10],[14,4,15],[11,15,3],[6,2,14],[6,11,8],[14,3,0],[14,15,9],[14,5,9],[14,4,3],[14,11,13],[8,13,14],[11,14,8],[6,12,14],[14,8,13],[12,13,15],[0,14,4],[14,12,6],[7,14,6],[14,7,13],[14,3,9],[14,0,8],[9,11,15],[14,9,4],[12,11,10],[14,2,15],[14,12,1],[15,6,14],[14,4,6],[14,0,4],[4,0,14],[8,13,14],[14,9,6],[13,14,9],[3,14,11],[10,1,14],[14,9,4],[14,1,0],[14,10,2],[3,7,4],[4,11,14],[14,11,4],[4,14,13],[0,14,11],[14,13,10],[4,5,0],[14,5,7],[15,1,14],[13,6,14],[2,15,0],[14,7,5],[12,14,3],[14,5,12],[4,14,10],[7,5,10],[5,13,9],[14,7,5],[13,5,14],[1,10,8],[14,5,11],[7,14,15],[2,5,14],[15,12,1],[14,6,11],[2,14,11],[14,12,6],[7,14,15],[14,5,15],[5,14,1],[14,11,1],[13,2,14],[14,11,5],[0,14,8],[9,10,5],[14,4,13],[11,14,9],[15,14,2],[14,1,9],[7,4,12],[13,8,14],[6,7,14],[14,15,0],[14,13,1],[14,3,11],[9,14,15],[14,4,10],[14,13,0],[14,0,9],[13,15,1],[14,3,11],[14,15,6],[14,5,0],[15,12,9],[14,15,13],[7,14,0],[14,13,12],[14,3,2],[1,9,14],[6,13,8],[14,9,11],[14,0,12],[5,14,4],[4,14,5],[7,13,8],[2,14,11],[0,14,12],[14,2,8],[1,6,10],[10,14,5],[14,5,8],[4,9,8],[11,8,9],[14,15,3],[14,10,13],[8,14,7],[11,3,7],[8,0,14],[15,6,11],[14,0,11],[9,14,1],[2,14,5],[1,6,8],[14,1,2],[14,7,15],[11,7,14],[11,3,14],[14,11,1],[14,3,0],[14,2,8],[14,8,5],[14,11,13],[0,14,2],[7,2,12],[4,14,15],[3,11,2],[14,3,12],[6,8,14],[4,15,14],[13,6,14],[2,0,12],[14,0,7],[14,8,6],[13,7,10],[14,8,9],[1,14,4],[14,15,3],[0,14,5],[7,14,12],[10,14,8],[14,4,0],[5,2,14],[5,14,12],[14,15,5],[5,13,1],[1,14,15],[13,14,8],[6,13,3],[14,15,0],[14,11,10],[8,14,2],[14,7,8],[15,12,1],[4,12,14],[14,0,10],[14,9,6],[14,4,0],[14,13,5],[14,1,12],[14,8,3],[14,12,10],[14,6,9],[14,13,3],[10,14,15],[12,4,2],[14,2,9],[9,14,1],[14,11,2],[2,4,8],[0,14,7],[14,6,7],[15,8,14],[14,1,5],[14,3,6],[14,1,11],[14,6,15],[14,12,10],[14,8,4],[5,15,14],[6,1,14],[6,14,4],[14,9,0],[14,8,6],[10,5,14],[14,12,9],[13,14,10],[14,3,8],[14,7,3],[7,9,12],[5,1,11],[14,15,12],[14,0,2],[14,11,6],[14,1,8],[6,14,8],[14,9,6],[1,14,6],[4,13,15],[14,1,10],[2,4,6],[13,14,1],[14,3,11],[14,7,2],[1,5,0],[14,11,5],[4,14,6],[14,4,15],[14,3,13],[14,10,2],[7,14,2],[15,11,13],[12,2,14],[14,12,1],[3,14,5],[2,9,14],[14,4,15],[2,10,14],[14,8,9],[7,15,13],[15,11,10],[14,5,10],[5,7,1],[14,6,9],[13,11,3],[14,12,13],[14,10,8],[14,15,10],[14,4,8],[14,10,6],[3,10,14],[14,9,11],[13,7,15],[14,8,4],[2,7,14],[8,4,14],[1,14,10],[14,0,8],[14,1,15],[6,14,1],[14,0,4],[14,3,11],[6,5,11],[2,14,12],[14,5,0],[0,6,14],[4,14,5],[11,14,5],[6,12,14],[14,5,4],[9,12,5],[9,3,14],[14,6,7],[4,14,10],[14,7,9],[14,7,3],[14,1,3],[5,7,14],[6,4,7],[11,4,14],[14,8,3],[14,10,0],[14,8,5],[3,14,4],[6,14,15],[14,10,15],[14,6,7],[5,11,8],[14,4,10],[14,1,8],[2,14,11],[11,15,0],[4,14,3],[3,15,14],[0,8,13],[14,10,12],[14,15,8],[14,1,2],[13,11,14],[12,14,10],[10,14,4],[14,10,0],[14,5,2],[14,12,1],[7,14,10],[6,14,12],[14,6,8],[14,12,5],[14,11,5],[14,2,1],[14,8,3],[14,6,9],[14,6,10],[4,14,9],[9,2,13],[3,1,0],[3,14,0],[15,14,11],[9,14,8],[5,14,7],[11,14,9],[14,10,4],[1,14,15],[10,13,12],[8,6,14],[0,14,2],[9,7,14],[5,14,13],[3,14,7],[13,4,14],[9,14,8],[2,14,8],[14,7,5],[14,3,13],[14,11,6],[14,12,2],[15,12,4],[11,13,8],[4,6,14],[13,14,10],[13,10,14],[14,12,7],[14,3,2],[14,12,1],[14,10,15],[13,7,14],[14,8,11],[7,14,11],[11,14,12],[7,14,11],[9,8,14],[14,7,2],[4,14,11],[2,14,15],[14,3,7]],[[14,0,8],[14,9,12],[6,14,9],[14,3,5],[10,14,2],[12,14,7],[14,9,4],[4,7,9],[5,3,14],[10,13,6],[9,7,10],[14,12,8],[1,14,11],[14,6,13],[14,3,4],[0,14,11],[10,14,0],[15,14,10],[14,7,10],[15,5,11],[14,3,10],[14,12,10],[13,8,14],[4,6,15],[14,5,4],[9,13,3],[14,3,9],[15,9,8],[5,14,2],[14,13,1],[14,4,13],[13,14,2],[13,10,14],[8,2,11],[0,12,14],[4,14,13],[14,0,2],[11,2,14],[7,10,14],[8,14,5],[5,14,1],[10,14,0],[3,5,14],[7,4,14],[14,6,9],[11,4,14],[1,14,7],[14,15,13],[9,4,2],[14,9,15],[9,5,3],[14,11,15],[8,14,0],[8,14,11],[2,13,14],[14,1,4],[14,0,2],[5,14,7],[9,0,14],[5,0,3],[12,10,4],[14,6,13],[7,1,6],[14,12,15],[4,14,3],[14,2,12],[14,12,4],[14,10,13],[14,4,15],[12,14,9],[3,14,15],[14,1,7],[14,1,11],[4,15,12],[14,10,7],[4,14,10],[3,7,14],[13,14,8],[14,2,12],[2,14,9],[11,13,14],[15,7,12],[14,2,10],[14,13,11],[8,12,14],[14,10,3],[7,12,2],[10,0,14],[0,1,14],[1,14,8],[0,3,14],[9,6,14],[14,5,1],[14,10,4],[14,0,2],[9,14,7],[14,11,5],[1,14,7],[14,2,5],[14,7,10],[9,14,13],[14,11,3],[9,10,14],[13,14,8],[6,15,14],[14,0,10],[3,14,11],[5,14,15],[14,9,0],[14,13,11],[14,0,5],[14,9,4],[14,15,12],[11,14,9],[7,14,4],[14,0,11],[14,9,0],[7,0,14],[14,9,3],[14,11,3],[14,0,12],[9,14,13],[8,5,6],[14,5,12],[14,4,5],[13,14,15],[12,3,9],[0,14,15],[14,12,3],[7,8,10],[5,8,14],[14,7,8],[0,11,14],[13,2,10],[14,13,2],[4,14,1],[7,14,11],[1,14,8],[8,3,15],[14,7,8],[2,9,7],[14,6,1],[9,14,7],[15,14,6],[14,2,3],[14,13,9],[14,3,12],[14,1,9],[14,10,13],[14,5,15],[14,4,15],[14,15,4],[13,3,10],[9,14,6],[0,5,14],[4,5,8],[8,14,10],[14,2,0],[14,3,6],[1,14,12],[4,14,10],[10,8,15],[15,1,14],[9,4,1],[13,14,8],[14,2,9],[10,14,12],[14,1,13],[14,11,15],[14,6,5],[5,8,6],[1,14,2],[15,5,3],[8,14,2],[0,15,7],[14,5,0],[4,3,14],[14,4,13],[14,15,3],[14,8,5],[14,2,8],[2,14,4],[3,14,4],[9,6,14],[14,15,1],[14,15,5],[14,13,1],[15,9,13],[14,15,8],[13,7,1],[12,14,11],[10,14,3],[14,15,9],[3,13,14],[1,14,12],[14,15,12],[7,10,14],[9,15,14],[3,14,12],[14,12,3],[14,4,8],[14,15,8],[14,12,8],[9,14,3],[14,9,1],[3,2,5],[14,15,9],[14,1,4],[14,10,1],[3,14,2],[13,6,5],[10,6,14],[14,8,4],[14,2,15],[8,3,13],[2,3,10],[14,5,0],[14,11,4],[3,14,1],[8,15,7],[2,14,11],[14,9,5],[0,7,14],[12,14,11],[14,15,10],[5,3,14],[14,15,6],[10,14,0],[1,14,7],[14,11,3],[14,10,9],[15,14,13],[1,15,14],[10,14,7],[14,0,13],[14,6,12],[3,14,1],[7,13,14],[8,9,5],[15,2,14],[14,2,0],[14,7,6],[14,1,13],[14,2,7],[14,7,2],[5,2,1],[12,11,14],[14,4,0],[0,14,10],[9,14,11],[5,14,11],[14,12,2],[10,9,6],[3,0,13],[14,3,0],[14,9,2],[13,14,5],[4,13,2],[14,6,10],[6,14,4],[14,11,1],[14,12,5],[14,1,6],[6,11,10],[12,3,14],[14,1,0],[13,1,11],[15,0,8],[7,14,4],[2,7,15],[12,2,13],[9,14,11],[0,14,9],[0,14,4],[14,10,2],[10,12,14],[1,14,3],[0,7,11],[13,14,12],[14,7,10],[13,14,6],[11,14,2],[14,10,0],[3,8,7],[14,0,7],[14,15,2],[11,3,14],[14,4,1],[14,11,13],[12,4,14],[8,14,5],[7,0,15],[14,5,4],[11,12,14],[7,11,6],[13,11,6],[14,7,13],[14,10,1],[7,13,8],[8,7,14],[13,14,12],[3,0,14],[15,10,14],[14,11,2],[12,6,1],[14,15,12],[14,3,15],[5,14,6],[14,10,12],[11,14,0],[14,9,2],[15,6,8],[13,3,8],[13,11,4],[14,3,0],[14,0,2],[10,14,15],[14,13,2],[15,10,11],[6,11,3],[8,2,12],[6,14,4],[6,11,14],[4,14,8],[2,15,14],[14,9,3],[14,10,9],[10,2,14],[4,14,3],[14,4,12],[1,14,10],[10,14,6],[14,8,6],[0,15,14],[15,14,10],[14,4,15],[14,10,11],[4,15,8],[8,14,0],[14,13,15],[10,14,6],[14,3,8],[14,6,9],[7,3,14],[14,0,9],[5,9,6],[15,14,6],[2,7,5],[13,5,14],[14,11,5],[5,4,13],[10,15,1],[14,9,12],[0,2,14],[14,9,10],[1,14,10],[14,9,15],[3,14,0],[2,14,8],[13,14,12],[13,15,14],[8,14,0],[1,14,2],[11,14,3],[14,3,4],[14,11,2],[3,13,1],[2,8,14],[4,14,12],[14,2,12],[14,7,12],[14,0,8],[11,14,4],[7,14,11],[8,2,6],[14,10,3],[14,9,7],[1,14,8],[14,6,4],[8,14,0],[12,3,14],[8,14,9],[5,14,3],[4,12,9],[5,14,6],[13,14,7],[7,14,12],[6,13,2],[11,14,13],[14,11,5],[14,7,11],[14,2,3],[14,6,1],[13,14,4],[14,15,9],[14,13,1],[15,14,13],[14,0,3],[6,14,7],[6,0,14],[14,7,6],[14,11,7],[14,15,7],[7,2,14],[4,12,15],[14,9,1],[14,4,9],[14,2,6],[0,2,14],[14,5,6],[14,8,12],[8,14,11],[3,14,2],[14,0,1],[8,15,14],[5,14,6],[0,14,13],[14,11,7],[7,14,15],[2,14,0],[7,14,6],[14,12,7],[5,9,14],[14,5,15],[14,9,0],[14,8,1],[1,14,6],[15,6,14],[0,13,14],[14,11,15],[2,1,12],[11,10,6],[6,14,11],[2,14,7],[14,15,6],[9,5,7],[2,14,13],[10,11,8],[6,14,8],[14,2,11],[14,4,3],[1,5,14],[3,14,1],[11,14,2],[3,14,6],[14,5,11],[10,14,7],[4,14,6],[14,8,6],[14,7,2],[8,11,5],[14,3,15],[2,3,14],[14,2,5],[15,8,1],[14,1,0],[14,12,2],[14,4,7],[8,14,4],[5,15,1],[1,14,12],[14,0,13],[8,14,7],[0,14,9],[14,3,6],[9,14,8],[5,14,6],[14,0,6],[13,14,6],[11,14,6],[11,14,1],[11,2,5],[14,8,12],[15,14,6],[3,14,12],[5,14,8],[14,5,4],[4,0,8],[14,11,3],[14,7,11],[2,14,9],[2,14,1],[14,15,1],[2,14,6],[10,14,6],[1,3,14],[9,8,0],[14,0,7],[14,9,3],[3,12,15],[1,9,14],[7,14,9],[14,11,15],[11,14,7],[14,8,9],[14,15,9],[14,4,15],[8,14,7],[11,12,10],[7,14,10],[15,11,8],[14,11,13],[0,10,7],[14,4,11],[11,14,3],[14,7,13],[5,4,10],[1,10,2],[11,3,14],[9,14,5],[14,5,12],[14,5,12]],[[5,14,0],[11,14,12],[1,13,14],[14,5,4],[4,9,6],[1,14,9],[1,13,11],[4,13,14],[14,2,9],[12,14,2],[14,0,9],[14,12,2],[0,4,15],[6,1,3],[8,14,10],[10,14,8],[7,5,14],[12,14,11],[2,9,8],[10,8,12],[2,1,15],[8,2,14],[14,13,11],[14,0,9],[7,14,3],[14,8,15],[7,9,14],[14,2,13],[8,6,5],[10,6,3],[14,15,7],[8,12,10],[14,11,4],[14,5,9],[14,2,4],[14,10,7],[3,1,14],[14,10,4],[14,15,5],[10,1,14],[14,6,2],[5,8,0],[3,9,4],[14,11,3],[14,11,4],[4,11,7],[14,6,2],[4,14,8],[14,10,5],[14,13,9],[0,14,2],[1,14,15],[7,14,10],[3,14,7],[14,8,4],[7,14,4],[0,14,2],[14,0,4],[4,14,1],[7,14,10],[4,14,7],[4,2,13],[14,0,8],[14,3,12],[14,13,12],[7,14,11],[14,4,12],[14,5,4],[12,14,6],[14,12,7],[10,15,0],[10,14,9],[12,3,14],[14,4,1],[14,13,9],[14,11,8],[7,13,14],[8,14,15],[14,8,9],[14,10,3],[14,10,0],[7,3,14],[5,1,3],[5,14,10],[7,14,6],[14,6,15],[5,14,3],[1,15,7],[7,2,6],[5,7,14],[14,4,12],[0,14,2],[1,3,4],[14,10,11],[2,4,14],[14,4,9],[14,0,4],[14,10,12],[9,0,14],[14,8,0],[8,4,14],[7,13,14],[14,1,2],[13,4,5],[14,4,0],[14,1,4],[15,14,0],[14,2,3],[11,7,8],[12,10,14],[7,10,3],[14,8,9],[14,2,11],[14,11,8],[11,14,7],[14,8,15],[2,14,6],[14,2,13],[3,6,15],[10,6,13],[14,10,8],[3,15,9],[14,11,12],[8,4,13],[6,14,12],[14,12,5],[14,0,10],[2,14,6],[14,10,4],[9,2,14],[14,4,1],[2,14,1],[6,14,15],[14,11,7],[2,14,9],[14,10,1],[14,3,9],[14,3,13],[14,0,11],[11,14,0],[7,10,1],[4,9,14],[15,9,5],[12,14,9],[12,14,4],[14,0,2],[14,3,5],[5,14,11],[14,2,15],[6,14,15],[12,15,10],[0,3,2],[0,6,14],[14,5,8],[14,13,6],[4,14,7],[14,3,4],[11,14,8],[15,6,14],[3,7,14],[11,8,15],[14,5,0],[14,7,9],[15,1,8],[5,14,9],[14,3,6],[7,0,11],[14,5,13],[14,4,13],[12,4,3],[14,12,2],[1,14,5],[5,11,14],[1,12,14],[10,8,12],[5,11,13],[9,1,4],[5,10,14],[14,4,12],[8,14,15],[14,0,5],[14,2,1],[4,14,15],[14,6,1],[8,14,6],[14,5,3],[13,0,14],[1,14,4],[8,14,13],[14,0,6],[13,10,11],[14,3,8],[0,9,14],[14,6,3],[3,14,13],[8,14,13],[14,8,0],[14,2,1],[4,1,0],[10,0,14],[14,5,12],[3,0,4],[7,14,8],[3,4,13],[14,11,3],[0,14,5],[8,13,11],[14,5,4],[13,14,0],[1,14,5],[10,14,0],[5,14,15],[14,13,9],[8,0,5],[4,14,7],[14,5,10],[14,10,15],[6,1,14],[0,14,4],[11,1,5],[14,2,8],[14,2,7],[3,5,8],[4,15,8],[11,6,2],[14,0,6],[14,13,15],[12,10,14],[14,13,4],[14,10,13],[14,15,12],[7,14,13],[11,8,10],[14,5,10],[3,14,4],[14,6,3],[8,14,10],[10,0,12],[5,14,12],[14,3,5],[6,1,0],[14,13,1],[14,1,8],[2,13,14],[4,15,14],[13,14,15],[14,4,9],[9,4,14],[10,14,0],[14,9,3],[14,6,0],[14,1,8],[10,3,13],[5,0,6],[10,13,14],[1,14,6],[14,6,10],[6,14,9],[14,1,4],[14,5,15],[14,13,3],[14,12,11],[14,11,5],[5,8,11],[1,14,0],[14,11,9],[14,3,6],[14,0,15],[14,3,5],[14,4,0],[7,9,4],[14,15,8],[8,1,14],[0,14,6],[14,9,6],[14,9,15],[4,14,9],[14,13,7],[14,8,2],[14,15,7],[2,12,14],[10,11,4],[7,0,14],[14,13,7],[11,15,12],[9,11,0],[14,8,10],[0,14,4],[11,15,14],[13,14,8],[7,2,14],[14,6,7],[2,14,12],[6,0,14],[4,12,14],[14,4,9],[8,14,10],[11,4,14],[14,0,4],[14,2,11],[3,14,4],[14,11,2],[11,1,8],[2,4,12],[4,10,14],[3,10,14],[6,8,14],[12,3,0],[14,12,8],[2,7,14],[2,10,1],[2,14,10],[15,0,9],[14,3,4],[15,12,2],[12,6,8],[9,13,7],[10,14,1],[14,8,4],[1,14,8],[14,6,12],[0,9,4],[14,9,7],[14,10,6],[14,7,15],[11,14,15],[14,15,3],[14,11,3],[4,14,12],[12,5,7],[12,6,15],[14,0,11],[9,12,5],[2,14,13],[4,14,1],[14,4,2],[14,0,5],[10,14,1],[3,14,8],[14,15,6],[14,0,13],[14,8,3],[10,14,11],[1,14,9],[14,6,0],[14,10,4],[14,3,4],[13,14,10],[14,12,10],[4,5,13],[14,12,9],[15,14,3],[1,11,14],[0,1,2],[10,14,8],[15,12,14],[7,4,9],[14,10,12],[14,2,13],[10,9,12],[14,7,8],[10,0,14],[14,8,12],[14,0,13],[13,4,5],[14,9,7],[14,7,0],[14,13,2],[14,6,9],[15,14,11],[8,15,6],[9,14,8],[9,15,14],[14,9,13],[14,4,13],[14,13,0],[14,5,2],[5,15,14],[8,14,1],[3,15,14],[14,15,8],[14,7,13],[14,3,12],[3,14,9],[8,15,13],[8,3,2],[14,9,12],[14,10,1],[1,12,14],[7,8,9],[14,0,6],[6,14,8],[14,9,0],[1,14,3],[14,5,3],[12,14,10],[6,11,1],[14,7,4],[14,6,2],[14,9,2],[8,5,6],[14,15,3],[14,9,15],[1,9,3],[14,1,15],[1,11,10],[14,4,11],[14,15,3],[11,15,4],[7,14,11],[14,2,12],[15,1,14],[6,1,14],[7,14,5],[9,14,7],[0,14,15],[14,8,9],[12,14,4],[14,7,5],[15,12,14],[14,3,1],[0,14,3],[5,14,8],[4,14,7],[14,9,1],[14,8,11],[14,5,9],[14,5,13],[4,10,5],[12,13,6],[8,14,11],[11,14,4],[12,14,8],[12,14,9],[14,1,15],[14,8,13],[11,14,5],[2,14,12],[10,0,15],[14,10,2],[13,14,15],[14,10,7],[13,0,4],[14,0,12],[14,10,3],[14,11,13],[15,14,9],[8,6,14],[0,14,13],[14,0,11],[14,12,8],[2,10,14],[14,2,15],[14,5,13],[12,14,4],[11,14,5],[14,3,15],[14,3,4],[4,14,5],[6,7,1],[5,1,14],[14,10,0],[14,12,0],[3,1,0],[6,14,1],[15,5,14],[14,10,7],[10,15,14],[14,15,12],[14,0,2],[14,3,6],[3,14,5],[14,12,13],[10,14,9],[15,12,11],[5,2,10],[10,15,14],[14,6,12],[8,14,3],[5,10,14],[12,13,14],[14,3,1],[0,1,13],[8,5,11],[14,2,8],[14,5,8],[14,9,0],[3,14,0],[14,8,3],[14,15,11],[14,6,15],[3,8,14],[10,3,2],[14,4,3],[14,4,11],[14,7,1],[14,9,5],[15,12,14],[14,7,9],[14,10,7],[2,0,10],[14,6,3],[15,12,14],[14,4,9],[10,14,6],[14,8,10],[3,4,14],[14,2,0],[1,5,14],[10,14,9],[14,2,4],[3,14,12]],[[14,9,5],[3,9,7],[9,14,11],[6,1,14],[14,9,1],[0,14,11],[3,5,15],[14,0,11],[5,8,7],[14,13,0],[12,6,10],[5,3,6],[15,14,9],[14,9,8],[14,12,8],[9,15,14],[8,14,13],[14,4,5],[1,14,9],[14,3,1],[14,4,7],[14,4,6],[14,7,2],[11,0,14],[14,3,5],[8,0,5],[14,3,7],[0,14,9],[4,14,10],[6,2,14],[10,14,13],[14,1,4],[14,7,10],[14,8,3],[9,14,5],[4,9,13],[14,12,2],[3,14,9],[4,6,14],[14,10,7],[14,8,3],[14,2,12],[0,14,7],[7,14,15],[14,5,13],[6,14,0],[4,7,14],[1,15,14],[15,5,1],[14,1,7],[13,10,14],[14,4,11],[14,12,6],[8,14,11],[15,14,0],[14,4,5],[13,11,8],[15,0,14],[14,9,0],[14,8,9],[2,0,15],[9,14,8],[3,6,14],[7,14,0],[14,10,13],[14,5,2],[7,15,5],[14,5,10],[14,6,10],[8,14,11],[13,8,11],[14,3,13],[3,12,14],[14,15,3],[12,14,7],[14,4,9],[11,13,3],[0,13,14],[14,2,5],[15,14,5],[14,7,10],[14,8,1],[14,5,10],[11,14,0],[14,6,5],[14,12,5],[14,11,13],[14,10,1],[2,6,14],[11,14,0],[14,9,4],[15,14,0],[2,10,12],[14,15,7],[14,7,12],[6,14,4],[14,7,0],[14,0,10],[14,2,11],[14,7,5],[14,9,7],[14,5,9],[12,9,14],[4,14,12],[14,1,15],[10,14,7],[14,2,6],[7,10,1],[14,3,12],[14,8,13],[14,15,8],[14,13,6],[14,3,6],[14,8,4],[14,8,9],[2,5,14],[7,5,1],[13,14,5],[1,14,15],[11,3,14],[2,0,11],[14,9,6],[11,14,3],[14,13,11],[12,9,6],[3,11,14],[14,3,7],[14,6,11],[14,3,11],[2,10,14],[12,14,3],[14,4,11],[11,1,2],[14,0,4],[14,9,2],[9,14,2],[14,3,7],[6,11,15],[4,13,14],[14,10,2],[14,9,10],[14,10,9],[14,4,15],[7,2,14],[14,15,7],[12,8,11],[13,15,14],[7,14,8],[15,5,14],[2,15,4],[14,8,2],[12,10,14],[9,14,3],[14,7,2],[14,2,4],[2,3,14],[12,10,14],[14,1,5],[2,10,14],[12,14,15],[14,13,6],[14,13,8],[14,15,12],[5,10,14],[9,14,13],[10,14,5],[3,14,8],[5,14,9],[8,14,13],[9,3,10],[4,9,14],[14,6,4],[14,12,11],[10,14,12],[14,6,7],[9,14,13],[7,2,1],[15,0,14],[5,14,2],[12,14,11],[14,2,11],[13,7,0],[11,13,3],[10,9,14],[11,0,14],[3,14,4],[4,3,1],[14,8,10],[14,3,2],[14,15,8],[14,0,6],[12,2,14],[15,3,0],[14,6,13],[1,10,12],[14,7,10],[12,14,0],[15,14,4],[4,14,10],[14,0,1],[4,9,14],[14,11,4],[14,8,13],[14,9,8],[14,2,1],[3,8,14],[7,6,14],[14,5,8],[14,0,7],[1,11,14],[5,4,3],[4,1,8],[9,14,13],[2,5,10],[14,5,15],[2,14,7],[14,10,13],[14,10,13],[13,0,14],[14,10,6],[8,9,13],[11,14,15],[7,1,14],[9,14,10],[14,11,13],[10,6,14],[9,12,14],[14,3,9],[8,14,12],[15,14,8],[13,14,4],[6,1,13],[14,15,12],[14,8,2],[8,1,14],[12,14,8],[8,0,14],[14,1,8],[6,3,13],[14,5,7],[11,14,10],[14,1,10],[5,14,7],[2,14,7],[7,2,1],[2,14,5],[1,0,7],[13,14,7],[14,4,12],[14,9,0],[3,14,11],[10,8,14],[0,14,7],[2,1,14],[14,12,10],[14,13,15],[1,14,15],[10,15,14],[14,3,4],[14,6,12],[14,12,9],[0,10,14],[14,7,12],[14,8,5],[3,14,7],[8,1,14],[14,13,9],[3,14,4],[14,6,0],[1,6,14],[0,14,4],[14,3,10],[11,14,1],[12,4,1],[6,14,13],[14,1,6],[14,6,7],[14,4,12],[8,14,11],[6,11,5],[1,3,11],[0,10,9],[4,14,11],[13,5,14],[1,14,9],[14,13,9],[4,15,14],[14,3,5],[14,13,4],[14,11,8],[14,3,4],[0,14,6],[14,4,0],[2,14,1],[14,2,0],[14,12,2],[14,2,0],[3,14,9],[14,10,4],[13,4,0],[14,1,9],[14,10,11],[4,14,5],[14,3,6],[1,0,14],[14,10,11],[11,14,10],[7,14,11],[10,14,0],[1,14,0],[14,5,8],[14,1,6],[13,14,1],[14,15,13],[7,2,5],[11,14,10],[8,14,11],[14,0,9],[10,6,14],[14,12,3],[14,4,10],[14,13,15],[13,0,11],[15,14,12],[14,4,0],[14,2,7],[10,12,14],[14,13,4],[12,9,0],[14,8,6],[1,14,0],[14,1,0],[0,10,14],[5,4,1],[14,3,7],[8,7,14],[14,7,15],[3,11,14],[4,1,14],[13,14,8],[14,0,13],[13,14,7],[15,14,6],[11,14,3],[14,11,10],[1,14,11],[14,6,15],[14,10,15],[14,4,8],[15,13,9],[14,13,1],[3,10,14],[14,1,6],[3,14,11],[4,1,5],[14,8,10],[3,14,9],[14,15,2],[14,11,13],[14,5,2],[4,13,6],[10,3,14],[8,14,3],[2,15,9],[2,8,5],[2,3,10],[13,14,8],[8,14,0],[14,7,12],[9,3,14],[14,6,3],[2,14,10],[14,8,3],[12,11,14],[9,12,14],[7,14,13],[15,8,14],[14,5,10],[5,14,15],[4,1,5],[14,11,6],[14,1,3],[6,14,11],[14,11,3],[14,13,3],[4,13,14],[5,14,2],[14,1,13],[3,7,14],[6,15,10],[9,14,11],[0,14,11],[12,6,4],[14,2,5],[4,13,14],[6,5,14],[14,11,15],[14,1,7],[3,4,14],[14,9,12],[2,14,1],[14,9,12],[10,8,14],[3,14,1],[4,14,12],[4,12,1],[11,14,10],[2,10,7],[5,14,9],[0,5,2],[14,15,1],[14,1,2],[2,13,14],[7,5,12],[14,8,12],[14,5,7],[1,12,3],[14,12,0],[12,14,11],[11,14,7],[14,6,8],[12,4,14],[9,5,14],[6,14,4],[15,10,14],[14,2,7],[4,6,14],[3,8,14],[14,12,8],[14,4,13],[5,14,0],[4,11,10],[10,8,7],[3,14,15],[14,10,8],[9,10,14],[1,10,14],[14,13,5],[14,9,5],[14,2,3],[2,7,14],[14,9,10],[13,2,14],[12,14,13],[14,11,3],[15,12,4],[10,14,4],[0,4,5],[5,12,14],[13,14,8],[8,14,9],[14,15,6],[5,14,13],[14,5,3],[6,14,12],[5,2,14],[15,14,4],[11,10,5],[0,7,14],[14,9,1],[2,14,10],[1,14,12],[14,6,5],[14,4,9],[10,14,7],[12,10,4],[14,9,0],[14,12,5],[10,12,14],[14,10,8],[1,14,6],[0,5,14],[10,9,14],[14,4,13],[9,7,14],[14,10,7],[14,4,10],[1,14,9],[14,12,3],[14,13,2],[2,3,14],[3,12,14],[0,14,1],[14,3,11],[1,6,4],[14,0,1],[14,1,4],[14,1,12],[6,3,14],[14,3,15],[15,14,4],[2,14,1],[14,12,3],[14,10,7],[14,4,12],[13,14,2],[14,1,13],[14,3,8],[14,8,4],[8,13,11],[4,14,5],[14,15,4],[2,15,13],[3,11,6],[14,9,4],[14,8,4],[3,14,11],[14,3,15],[14,1,11],[12,10,14],[14,1,4],[7,0,8]],[[14,13,7],[14,0,8],[9,14,6],[12,14,5],[5,14,4],[10,14,8],[15,14,5],[14,5,13],[4,3,12],[10,12,7],[1,4,13],[3,14,15],[14,15,3],[14,7,3],[14,0,9],[10,5,13],[5,14,10],[4,15,14],[14,6,4],[14,12,4],[14,3,15],[14,4,2],[2,6,14],[14,5,11],[14,2,10],[15,14,3],[15,10,14],[4,0,2],[4,12,15],[8,9,12],[14,2,12],[14,1,8],[6,14,9],[9,4,14],[14,9,5],[14,13,4],[14,10,5],[14,3,1],[14,5,11],[14,4,0],[7,14,1],[6,14,13],[8,14,3],[6,14,7],[1,14,11],[4,14,2],[2,3,11],[10,11,6],[13,9,14],[14,11,2],[13,14,11],[14,12,0],[14,1,8],[14,13,3],[11,14,10],[14,11,1],[14,9,1],[7,4,14],[14,5,15],[9,10,0],[14,5,3],[3,4,14],[14,12,0],[8,10,5],[14,13,4],[15,14,6],[1,14,9],[14,12,9],[10,4,14],[5,14,2],[2,11,8],[3,8,5],[14,9,5],[14,3,2],[9,7,14],[0,14,10],[11,14,9],[14,6,15],[9,14,1],[14,9,4],[13,14,9],[14,3,1],[14,7,3],[11,12,13],[15,4,14],[14,4,6],[14,13,11],[12,4,3],[11,14,8],[5,14,11],[7,2,14],[1,8,13],[11,0,14],[0,6,1],[4,14,12],[14,5,12],[14,2,13],[2,7,11],[15,5,10],[1,12,14],[14,13,11],[3,2,5],[14,5,7],[3,14,4],[14,13,3],[0,1,14],[10,8,14],[8,5,14],[15,0,5],[15,14,11],[15,14,0],[9,1,12],[14,2,15],[13,14,3],[14,9,1],[14,6,3],[14,15,1],[14,12,6],[12,10,14],[6,1,11],[8,4,0],[14,5,1],[3,15,14],[2,13,0],[14,5,1],[6,12,14],[7,8,14],[7,14,11],[14,3,5],[14,0,15],[12,14,5],[14,4,11],[14,15,1],[14,6,7],[6,9,13],[0,4,3],[14,11,6],[8,10,1],[14,7,3],[14,15,5],[2,13,12],[14,3,2],[14,4,13],[7,14,0],[14,6,0],[14,1,10],[10,14,4],[14,10,9],[14,4,12],[14,10,15],[14,12,3],[14,9,4],[14,4,15],[12,14,15],[14,1,5],[14,12,13],[14,5,12],[14,15,7],[14,9,2],[14,7,15],[2,14,10],[15,14,2],[14,0,6],[4,14,0],[15,9,14],[11,7,13],[13,7,3],[14,4,15],[5,11,14],[14,5,11],[14,2,10],[14,6,10],[14,6,8],[11,13,14],[15,0,14],[3,14,1],[14,13,12],[1,3,14],[15,14,10],[14,0,15],[14,5,13],[1,14,15],[14,8,9],[14,1,13],[11,10,14],[10,14,0],[9,15,14],[14,5,7],[0,12,7],[14,3,9],[2,14,4],[14,6,11],[11,5,14],[8,3,14],[5,13,11],[14,5,10],[8,14,2],[9,14,13],[8,14,1],[2,3,14],[14,9,10],[14,2,10],[14,10,8],[4,13,5],[4,14,12],[8,14,5],[13,8,14],[5,13,11],[9,8,14],[12,9,14],[14,3,11],[3,14,4],[8,3,14],[6,15,14],[4,14,0],[14,8,12],[14,2,10],[1,15,14],[11,15,14],[8,14,10],[14,2,9],[6,9,5],[9,4,14],[14,11,1],[12,7,14],[14,4,13],[1,7,4],[14,13,15],[8,0,15],[14,3,13],[1,14,15],[0,14,2],[14,2,11],[9,14,1],[14,12,8],[1,8,9],[14,3,8],[11,14,12],[13,0,14],[6,14,13],[4,14,12],[12,14,1],[14,6,10],[2,14,10],[14,13,3],[8,13,7],[13,14,7],[14,7,2],[8,14,1],[4,15,14],[5,14,1],[8,14,1],[1,14,6],[0,13,14],[7,14,9],[14,10,2],[14,8,13],[15,5,12],[14,9,11],[8,7,14],[7,13,11],[11,14,3],[12,14,3],[11,14,15],[15,10,2],[14,3,10],[2,14,8],[6,14,10],[15,14,10],[6,9,14],[14,13,8],[14,3,7],[14,15,1],[12,15,4],[7,14,5],[14,13,8],[13,8,9],[2,0,4],[14,3,10],[10,15,7],[14,10,13],[14,0,1],[6,0,10],[5,9,0],[14,11,10],[14,0,7],[12,13,14],[14,8,4],[14,1,2],[10,14,6],[3,14,1],[14,8,11],[2,12,14],[15,1,14],[14,10,4],[14,2,5],[14,6,1],[5,13,14],[14,15,0],[1,10,14],[1,3,14],[11,13,3],[12,14,0],[2,11,10],[11,14,1],[5,14,7],[8,0,10],[5,0,1],[0,14,15],[14,12,4],[14,7,0],[14,1,0],[13,3,14],[0,14,10],[14,10,7],[14,13,3],[12,14,0],[14,1,6],[0,14,12],[11,14,2],[9,14,10],[14,11,7],[10,14,2],[14,11,9],[14,6,4],[8,9,14],[14,10,5],[2,5,13],[3,0,7],[14,10,4],[14,12,15],[6,14,1],[14,4,13],[14,8,15],[13,14,10],[8,14,10],[14,13,7],[10,7,14],[3,14,15],[9,1,14],[0,14,12],[14,5,1],[14,9,4],[14,13,8],[14,8,12],[8,11,5],[8,12,14],[5,14,9],[2,14,1],[14,9,8],[14,8,9],[1,14,9],[14,7,13],[9,4,0],[14,1,2],[7,14,5],[8,1,14],[14,0,3],[14,10,15],[14,4,13],[7,4,14],[5,15,14],[14,0,12],[14,15,3],[14,3,11],[14,11,4],[14,13,4],[14,12,1],[13,6,7],[14,12,6],[14,1,5],[14,7,10],[8,14,2],[12,0,14],[12,14,9],[14,8,3],[9,5,11],[10,14,15],[14,6,15],[7,14,1],[10,14,2],[14,1,6],[14,8,9],[14,4,11],[14,1,3],[14,10,13],[14,1,4],[8,12,14],[14,4,15],[13,14,0],[3,5,14],[7,14,9],[14,3,6],[6,14,3],[12,14,15],[14,11,3],[3,14,5],[14,11,10],[14,5,2],[14,5,6],[0,3,4],[9,5,12],[14,15,0],[9,14,6],[3,0,14],[3,14,0],[5,14,1],[14,5,7],[0,14,3],[8,13,6],[1,14,0],[4,14,0],[4,0,14],[0,13,14],[14,4,0],[8,14,11],[14,1,9],[8,14,2],[14,9,4],[3,14,1],[1,14,4],[14,15,10],[6,14,15],[1,8,14],[14,10,0],[13,14,10],[14,3,8],[14,8,2],[14,2,10],[14,1,4],[2,9,6],[0,14,1],[14,0,11],[13,8,4],[14,7,6],[14,4,10],[14,11,1],[14,8,6],[1,14,15],[5,14,8],[3,6,14],[10,9,7],[14,10,4],[5,11,14],[0,14,4],[14,5,1],[10,11,14],[14,1,7],[14,12,9],[7,10,0],[6,2,14],[14,8,2],[14,8,11],[3,14,8],[14,11,10],[14,5,9],[14,4,12],[14,10,11],[14,8,5],[7,8,3],[14,7,9],[14,8,7],[8,3,14],[3,6,8],[15,3,8],[11,14,4],[14,0,2],[14,10,4],[14,1,6],[3,4,6],[14,12,11],[15,9,14],[13,8,14],[8,13,1],[4,9,14],[11,1,14],[14,12,13],[14,13,12],[13,14,11],[10,8,14],[4,13,14],[2,12,1],[14,9,10],[14,15,11],[15,9,7],[14,5,0],[14,1,11],[11,14,13],[3,14,1],[5,14,11],[14,11,3],[10,3,15],[14,7,15],[1,14,2],[15,14,5],[14,5,15],[14,15,13],[12,10,3],[14,1,7],[1,14,9],[8,1,14],[13,15,14],[14,1,3],[5,6,14],[2,14,5],[7,0,14],[2,14,7],[14,7,8],[7,14,2],[5,1,11],[14,13,9],[14,15,1]],[[10,5,2],[15,14,6],[14,7,3],[14,6,8],[6,14,8],[9,0,13],[14,2,10],[14,10,9],[13,14,11],[14,3,13],[14,10,4],[14,8,10],[14,2,15],[5,14,3],[12,14,11],[14,0,2],[9,14,13],[14,11,6],[12,5,10],[15,14,6],[15,2,10],[14,6,7],[5,14,9],[2,10,14],[8,14,9],[14,4,13],[14,0,13],[14,2,4],[14,4,2],[1,15,0],[14,4,6],[0,7,11],[14,15,7],[11,14,8],[14,10,12],[2,14,7],[11,5,14],[14,9,2],[13,14,10],[4,14,1],[2,4,6],[10,14,6],[5,14,12],[11,2,14],[14,11,0],[15,7,3],[11,1,14],[11,14,2],[0,14,3],[14,0,5],[14,10,6],[10,1,14],[1,14,6],[9,15,12],[4,13,14],[5,15,11],[14,0,8],[8,14,2],[14,6,12],[7,14,0],[14,3,8],[14,13,8],[3,14,6],[14,12,6],[8,0,5],[6,14,10],[10,14,5],[4,2,14],[14,15,2],[1,14,4],[6,5,11],[14,4,0],[13,14,15],[14,10,3],[8,5,3],[6,13,14],[8,14,2],[14,15,1],[2,3,14],[8,14,13],[14,8,15],[14,13,9],[3,14,4],[7,14,8],[14,1,8],[11,4,14],[5,14,11],[14,9,7],[12,3,8],[7,14,1],[8,14,10],[14,0,6],[14,11,3],[14,12,11],[14,4,13],[3,9,14],[1,15,14],[14,2,9],[11,4,14],[7,14,4],[14,11,9],[15,9,4],[14,3,13],[14,0,15],[11,14,0],[1,10,3],[0,14,13],[14,9,10],[14,5,2],[13,6,7],[14,9,8],[14,9,7],[2,1,14],[6,14,1],[0,3,1],[4,2,1],[14,13,15],[14,1,10],[7,14,11],[14,15,12],[14,13,12],[9,14,0],[12,7,8],[1,0,4],[14,0,6],[14,4,7],[4,1,12],[14,7,3],[3,14,4],[1,14,3],[14,1,6],[14,12,13],[14,0,5],[14,1,9],[14,8,13],[14,12,13],[4,14,5],[2,6,12],[9,10,14],[8,14,1],[1,3,2],[4,0,14],[14,6,15],[2,5,10],[13,8,3],[12,10,14],[4,5,14],[7,10,14],[1,2,14],[10,14,2],[6,4,11],[12,14,3],[10,14,5],[8,14,7],[7,3,12],[14,13,10],[10,7,14],[9,12,15],[11,10,7],[11,14,10],[5,14,3],[14,9,0],[14,8,3],[2,9,13],[14,5,11],[14,13,10],[14,2,8],[5,13,7],[8,10,14],[14,5,12],[15,14,3],[14,4,6],[14,10,6],[14,10,9],[14,11,9],[10,14,3],[7,14,13],[15,14,2],[14,9,7],[14,9,4],[14,2,9],[13,12,3],[0,6,14],[14,11,1],[4,13,15],[0,14,8],[11,2,14],[12,11,3],[8,0,3],[14,5,11],[5,11,0],[14,12,4],[5,3,11],[8,14,10],[14,10,11],[6,14,8],[8,12,14],[6,3,11],[4,5,2],[14,4,2],[6,14,3],[14,10,2],[9,14,2],[14,9,10],[15,10,0],[10,14,7],[3,14,6],[4,14,7],[6,9,15],[9,10,11],[14,3,8],[12,14,5],[13,14,11],[9,14,5],[14,1,4],[11,12,2],[11,0,14],[8,0,14],[14,3,7],[14,4,12],[6,4,14],[5,4,6],[14,3,5],[14,7,4],[10,14,12],[12,8,4],[14,5,9],[14,2,11],[14,7,10],[14,10,0],[14,9,10],[10,9,14],[13,11,6],[14,13,15],[14,1,2],[14,7,9],[14,15,6],[8,14,5],[5,14,11],[9,14,6],[9,14,8],[10,14,2],[14,10,8],[12,9,4],[1,0,15],[6,10,0],[14,15,8],[13,11,1],[1,5,14],[14,11,1],[14,11,10],[14,3,0],[14,2,9],[15,14,6],[4,14,8],[5,10,1],[15,14,10],[1,14,8],[14,11,0],[14,7,5],[12,14,1],[14,9,1],[14,15,12],[1,15,11],[3,14,0],[14,6,11],[11,14,4],[10,14,12],[14,8,5],[14,0,8],[12,1,8],[14,9,6],[3,11,10],[14,7,2],[14,13,1],[14,11,10],[14,13,15],[14,13,7],[0,10,6],[11,12,1],[14,12,8],[6,13,4],[14,5,6],[1,14,13],[0,6,9],[14,9,2],[8,14,13],[8,14,10],[15,14,5],[0,14,15],[3,8,14],[14,4,6],[14,7,8],[14,10,9],[14,6,7],[12,14,13],[14,7,12],[15,14,4],[9,14,2],[8,14,11],[8,14,6],[14,3,12],[14,7,15],[15,10,11],[14,0,10],[14,7,9],[14,7,6],[14,6,10],[14,6,10],[8,7,15],[14,0,11],[10,14,13],[7,14,13],[1,7,14],[14,13,7],[1,5,8],[2,6,3],[14,2,0],[13,14,8],[14,1,7],[9,6,14],[5,14,10],[9,14,6],[5,4,14],[14,1,11],[12,1,6],[5,8,15],[8,9,14],[15,5,14],[13,5,1],[10,14,4],[14,8,1],[7,1,15],[14,8,7],[14,2,13],[0,12,14],[14,1,2],[9,14,6],[14,5,1],[13,8,3],[1,8,14],[8,3,9],[13,14,10],[13,14,10],[14,9,5],[14,8,2],[14,9,0],[14,9,7],[10,9,2],[13,14,15],[2,10,14],[13,7,1],[14,15,6],[14,8,0],[4,11,14],[3,14,1],[1,7,14],[14,3,5],[5,14,1],[14,12,10],[12,14,5],[14,12,9],[9,5,14],[0,4,10],[4,7,5],[10,6,14],[15,14,10],[12,14,8],[14,10,7],[5,12,14],[14,1,13],[14,4,8],[14,8,10],[1,6,14],[13,1,14],[14,3,13],[14,9,0],[14,13,10],[14,4,12],[14,12,8],[14,15,13],[14,13,1],[14,2,0],[13,11,3],[14,2,15],[14,15,12],[0,14,1],[14,7,12],[14,4,2],[14,1,4],[12,14,8],[8,14,11],[1,2,14],[4,14,8],[13,9,6],[11,6,12],[14,7,2],[14,5,4],[11,1,3],[0,1,14],[6,14,10],[5,9,15],[14,15,3],[14,7,13],[14,3,5],[14,5,8],[14,7,6],[14,9,1],[14,11,13],[14,0,7],[9,14,3],[0,14,2],[14,11,1],[1,9,14],[14,13,1],[8,14,7],[6,1,14],[14,7,0],[14,0,4],[3,7,14],[0,7,14],[10,14,8],[6,14,12],[14,9,0],[14,6,9],[14,0,2],[0,14,10],[14,6,4],[4,14,3],[13,5,10],[12,14,1],[14,13,5],[14,6,9],[10,14,5],[14,13,3],[7,11,14],[15,14,8],[12,7,8],[14,6,1],[15,7,14],[14,4,11],[1,9,15],[14,4,7],[15,14,8],[9,14,7],[14,11,0],[14,13,10],[10,4,14],[14,7,0],[1,13,14],[14,11,10],[14,0,2],[10,14,0],[8,14,0],[3,11,14],[2,14,6],[8,13,3],[10,13,8],[4,11,14],[14,3,5],[14,5,2],[8,9,6],[15,13,14],[2,14,13],[10,7,1],[14,12,10],[0,6,15],[6,14,10],[1,14,7],[14,5,4],[14,8,11],[15,9,14],[8,14,2],[14,8,7],[4,14,6],[14,8,1],[14,3,8],[6,2,7],[7,14,12],[11,10,1],[14,2,4],[14,7,11],[14,3,8],[6,14,7],[14,9,1],[8,6,14],[14,8,13],[2,13,4],[14,10,0],[14,9,11],[14,2,7],[14,4,15],[8,5,14],[14,7,8],[15,1,5],[10,14,7],[9,14,2],[4,1,14],[0,14,3],[14,5,3],[0,14,13],[14,4,2],[14,2,13],[11,5,14],[14,3,8],[14,11,1],[0,8,15],[12,15,14],[5,11,8],[14,4,10],[12,14,15],[2,14,1]],[[14,11,4],[2,14,10],[14,5,4],[9,14,1],[15,14,1],[4,14,3],[13,0,2],[2,14,1],[14,12,10],[14,8,11],[9,13,14],[14,15,11],[11,8,9],[14,11,2],[14,5,4],[3,1,14],[14,9,10],[13,14,7],[7,14,5],[15,14,10],[0,14,11],[14,3,8],[15,14,11],[14,7,3],[15,14,12],[14,1,9],[14,3,6],[2,9,5],[6,14,7],[11,14,6],[14,11,15],[12,3,6],[14,8,7],[14,5,3],[8,14,2],[14,4,1],[8,2,0],[14,2,8],[14,9,0],[14,9,8],[3,14,12],[14,7,10],[12,11,14],[6,11,9],[9,15,4],[5,14,1],[9,2,7],[11,14,2],[14,4,5],[14,5,6],[12,14,15],[14,11,13],[15,14,5],[13,1,14],[14,3,12],[15,14,7],[14,3,5],[11,3,14],[14,3,2],[3,8,0],[14,13,1],[14,0,15],[14,10,15],[14,13,10],[14,1,15],[14,1,13],[12,14,0],[14,11,6],[14,3,4],[8,7,0],[14,12,5],[14,6,4],[14,0,5],[14,13,0],[5,14,9],[15,9,14],[12,7,6],[11,14,12],[14,6,10],[14,1,12],[6,14,15],[5,12,8],[14,2,5],[14,4,10],[14,15,10],[14,0,9],[0,7,6],[2,13,14],[13,14,3],[14,3,2],[14,3,2],[12,14,6],[7,14,8],[14,7,1],[14,6,0],[14,10,7],[15,14,10],[3,1,9],[14,6,10],[14,9,15],[14,11,1],[13,2,14],[14,7,12],[14,10,3],[14,1,2],[2,14,5],[8,14,11],[14,13,5],[14,0,15],[9,14,12],[10,4,3],[10,14,4],[15,14,1],[3,14,0],[14,3,0],[9,14,3],[14,8,12],[3,15,14],[4,0,13],[14,0,2],[3,5,11],[8,13,10],[14,7,4],[14,6,8],[15,14,11],[14,10,11],[12,7,2],[9,2,5],[14,15,10],[0,10,3],[11,14,3],[15,5,11],[14,10,3],[14,15,1],[14,1,11],[10,14,12],[8,12,14],[14,10,0],[7,11,14],[13,14,11],[10,14,4],[14,4,15],[5,4,14],[1,10,14],[15,0,14],[14,2,13],[9,0,14],[14,10,0],[14,12,0],[6,8,15],[7,14,11],[14,11,13],[4,7,14],[14,1,10],[10,14,11],[4,0,11],[4,14,8],[14,7,8],[13,14,3],[4,8,11],[15,11,6],[14,8,12],[11,13,3],[14,11,7],[13,15,8],[6,14,3],[14,2,7],[14,13,15],[14,2,3],[12,14,2],[14,7,5],[8,2,14],[10,5,14],[14,15,4],[6,14,11],[11,14,5],[6,13,9],[4,1,12],[1,14,12],[9,6,14],[12,1,14],[3,4,7],[14,0,1],[14,15,11],[12,9,7],[7,14,10],[14,0,15],[14,1,12],[14,12,4],[4,3,15],[8,11,14],[14,8,1],[14,12,6],[14,13,5],[8,7,13],[14,8,6],[0,14,1],[14,0,6],[2,14,8],[14,8,10],[14,6,5],[14,7,2],[14,6,11],[14,4,9],[5,0,15],[14,11,13],[15,14,6],[14,11,5],[14,10,15],[14,3,12],[14,9,13],[14,13,2],[6,7,13],[0,14,1],[14,12,3],[14,2,5],[6,14,3],[3,9,10],[10,9,13],[15,8,0],[14,15,13],[8,1,2],[14,7,10],[14,4,2],[10,14,3],[14,3,6],[4,14,10],[14,3,8],[12,14,9],[11,14,2],[14,13,6],[14,6,11],[14,10,13],[4,15,14],[14,9,15],[10,14,3],[14,3,2],[7,11,14],[4,14,13],[14,5,11],[14,6,8],[15,9,2],[3,14,5],[14,13,8],[14,3,13],[2,14,9],[7,14,6],[1,3,0],[14,12,1],[0,9,11],[11,9,4],[5,14,15],[14,12,2],[8,2,10],[11,14,0],[10,8,9],[10,14,2],[14,11,9],[6,9,14],[14,9,2],[14,0,11],[14,9,5],[14,13,2],[7,8,12],[0,6,11],[14,9,6],[14,13,9],[6,14,5],[7,13,14],[14,0,2],[13,12,6],[15,14,5],[14,11,4],[14,12,1],[9,14,2],[7,5,4],[14,4,3],[0,12,8],[14,9,1],[4,1,7],[14,5,7],[7,14,12],[14,10,15],[5,14,3],[14,3,11],[14,15,12],[15,5,11],[14,1,12],[9,6,14],[15,14,6],[14,5,0],[14,8,3],[0,11,10],[14,6,3],[14,3,11],[14,4,0],[14,9,4],[4,8,0],[14,7,8],[14,11,4],[14,4,11],[4,1,9],[14,1,0],[14,1,5],[8,14,13],[13,11,4],[1,14,13],[14,6,3],[3,14,5],[14,10,6],[0,14,2],[14,11,10],[12,13,14],[14,9,7],[0,14,12],[14,15,12],[1,14,2],[7,14,4],[9,4,13],[7,2,8],[14,8,1],[12,14,9],[15,10,14],[14,3,13],[9,2,14],[7,8,3],[2,14,5],[14,9,1],[14,6,4],[9,10,14],[4,8,9],[14,13,15],[14,12,11],[3,6,14],[14,10,6],[4,14,10],[14,15,10],[12,14,8],[2,14,5],[14,7,13],[14,9,10],[14,2,8],[15,14,10],[14,10,5],[2,14,8],[4,14,5],[2,0,6],[0,14,13],[14,6,3],[0,4,14],[14,15,3],[8,14,15],[9,1,14],[14,10,7],[5,8,14],[8,6,12],[14,7,8],[6,15,14],[4,12,3],[5,15,14],[2,6,14],[14,3,9],[14,1,8],[14,10,4],[14,15,2],[8,10,3],[7,14,8],[15,14,5],[14,5,3],[5,14,0],[15,14,11],[12,2,5],[13,14,15],[14,8,1],[4,12,1],[14,2,0],[14,8,2],[8,15,14],[14,5,4],[14,0,9],[13,1,3],[9,14,2],[14,4,6],[0,14,4],[14,1,2],[12,3,14],[6,1,2],[4,13,12],[9,1,4],[9,14,15],[12,6,0],[9,8,14],[13,14,7],[14,1,13],[14,7,4],[12,14,1],[12,15,5],[13,12,14],[14,8,4],[14,7,11],[14,11,6],[6,8,14],[14,13,5],[5,2,11],[9,5,13],[8,14,12],[3,15,14],[12,0,15],[12,10,14],[11,14,9],[14,4,6],[14,15,12],[14,10,11],[14,5,6],[14,13,8],[14,1,13],[14,13,7],[14,15,8],[13,14,11],[8,14,4],[11,0,14],[12,14,5],[14,2,4],[6,14,7],[10,14,0],[14,2,10],[10,14,3],[13,14,2],[1,14,6],[7,14,2],[6,14,9],[14,5,1],[8,9,14],[1,14,8],[14,2,11],[14,10,4],[14,10,0],[14,1,6],[2,11,10],[14,4,0],[15,6,14],[14,11,4],[2,13,14],[7,13,8],[14,2,5],[6,7,14],[0,14,2],[14,2,1],[14,13,7],[6,14,0],[14,12,11],[14,10,12],[3,10,14],[14,0,12],[10,2,14],[2,14,4],[14,9,12],[9,15,14],[14,15,9],[1,12,7],[14,6,15],[14,1,15],[14,9,3],[5,9,2],[14,11,1],[2,14,1],[14,2,6],[14,4,3],[13,14,8],[9,8,14],[14,13,1],[8,1,4],[14,2,13],[14,13,9],[9,4,10],[1,6,10],[14,0,1],[5,14,9],[0,14,10],[14,13,12],[14,12,6],[0,14,8],[14,5,11],[12,14,9],[14,8,7],[6,3,14],[14,15,1],[3,14,8],[14,12,10],[13,3,14],[14,8,10],[9,14,4],[15,10,14],[15,8,7],[2,14,8],[1,14,13],[5,9,10],[14,2,0],[14,12,9],[15,2,14],[14,2,0],[14,10,4],[0,14,8],[4,9,11],[12,6,14],[14,8,10],[13,14,4],[5,4,8],[3,15,4],[11,14,2],[5,13,14],[14,3,6]],[[10,14,6],[12,14,10],[14,1,6],[12,14,10],[14,4,10],[0,14,10],[14,3,7],[14,13,7],[13,7,0],[11,14,5],[10,14,11],[0,4,14],[1,5,14],[13,15,14],[12,10,14],[11,13,5],[14,2,0],[11,12,14],[7,14,0],[14,5,12],[14,12,11],[14,6,10],[11,14,12],[14,4,3],[14,12,4],[14,8,12],[8,14,9],[14,3,1],[3,14,8],[14,9,3],[8,5,14],[14,10,4],[14,8,2],[4,14,12],[5,14,3],[14,4,11],[12,14,11],[13,14,0],[14,5,10],[5,0,15],[14,10,6],[11,14,15],[5,14,3],[14,5,11],[15,1,11],[1,14,7],[10,1,14],[14,12,11],[5,14,6],[0,5,4],[14,9,4],[14,4,3],[0,14,15],[7,11,12],[14,5,15],[14,7,0],[6,13,1],[14,4,7],[14,10,9],[13,14,5],[14,3,13],[14,2,6],[14,6,5],[14,3,11],[14,3,13],[14,4,2],[10,11,1],[14,13,7],[14,6,15],[9,14,3],[14,2,8],[3,14,0],[14,0,9],[14,9,6],[14,13,15],[11,1,14],[14,6,1],[14,7,6],[5,15,8],[14,3,0],[7,2,3],[9,8,10],[3,14,7],[12,14,0],[14,6,10],[0,13,12],[11,14,3],[14,13,1],[3,14,9],[13,14,4],[2,14,11],[2,8,4],[0,14,13],[14,11,4],[2,14,4],[14,0,3],[14,10,7],[6,15,14],[1,2,12],[2,14,3],[11,14,15],[13,14,15],[7,14,12],[14,13,12],[14,10,5],[14,8,2],[2,9,14],[5,2,14],[15,14,6],[5,14,15],[14,15,7],[8,14,1],[3,10,14],[6,0,15],[14,13,0],[8,3,4],[14,5,15],[8,9,14],[2,3,14],[14,4,6],[1,14,9],[12,14,2],[2,14,11],[13,1,6],[4,14,12],[14,6,3],[14,5,0],[3,14,9],[0,14,11],[10,5,14],[15,12,7],[6,12,14],[14,12,7],[14,15,1],[12,14,8],[14,2,12],[14,4,0],[8,10,11],[14,8,6],[0,14,3],[6,14,12],[2,14,12],[14,10,3],[14,10,7],[14,10,3],[14,4,15],[14,1,6],[14,0,10],[1,11,2],[14,7,12],[15,11,14],[14,10,13],[1,14,9],[14,3,13],[13,5,0],[1,14,2],[14,7,13],[14,11,6],[6,4,8],[9,10,15],[0,14,12],[12,3,14],[14,3,0],[3,0,1],[14,15,5],[9,5,15],[9,14,12],[14,4,5],[5,7,14],[13,14,12],[14,12,1],[14,8,11],[14,0,9],[14,5,11],[14,10,2],[14,7,8],[14,2,3],[5,3,14],[6,2,5],[15,5,14],[0,4,14],[14,10,9],[0,13,2],[8,14,4],[1,6,5],[14,9,5],[10,14,9],[2,14,3],[1,14,9],[2,11,14],[12,4,14],[12,11,0],[9,4,12],[14,10,1],[6,14,13],[14,4,2],[2,14,6],[11,14,12],[1,11,14],[14,8,4],[6,11,0],[14,9,15],[14,7,4],[8,10,12],[12,14,8],[3,10,14],[14,5,10],[7,9,14],[14,3,2],[3,7,10],[14,11,4],[14,2,15],[11,14,12],[13,14,10],[7,14,0],[1,14,11],[13,14,0],[1,12,14],[1,0,14],[9,11,14],[13,14,3],[14,15,10],[8,14,1],[12,14,0],[5,14,4],[14,9,10],[4,11,14],[14,2,3],[9,13,14],[1,8,9],[14,15,2],[10,14,8],[14,7,0],[8,14,1],[14,2,10],[7,14,0],[2,10,6],[14,4,1],[15,2,14],[14,4,2],[12,14,10],[14,11,3],[14,0,6],[14,6,13],[13,14,5],[12,15,14],[14,6,13],[4,1,14],[5,3,14],[14,5,2],[12,14,3],[0,14,6],[7,14,2],[14,11,3],[14,9,10],[10,11,14],[14,1,8],[3,14,7],[11,14,12],[14,15,3],[14,11,3],[14,3,11],[14,11,12],[14,0,1],[14,9,11],[4,11,10],[14,9,10],[7,14,11],[13,15,10],[14,6,8],[14,1,10],[14,13,6],[14,15,8],[7,14,9],[10,14,5],[14,2,6],[5,14,6],[14,7,12],[14,10,15],[10,14,0],[14,12,8],[14,3,9],[14,11,1],[4,14,6],[14,11,9],[0,14,10],[14,2,3],[1,14,4],[1,8,14],[14,5,3],[15,14,13],[14,5,13],[14,0,7],[14,15,9],[14,15,0],[11,5,12],[12,14,15],[12,14,6],[11,2,14],[8,0,14],[14,9,0],[9,14,4],[14,10,13],[9,14,5],[14,5,0],[6,4,14],[14,1,0],[14,8,9],[0,14,6],[1,14,11],[6,14,11],[14,4,11],[8,14,10],[3,14,0],[13,10,1],[5,3,14],[5,8,12],[14,10,3],[14,6,2],[14,7,10],[14,3,1],[14,1,15],[14,4,0],[14,1,2],[14,1,15],[15,14,4],[13,14,4],[14,12,2],[13,14,3],[14,12,8],[7,14,1],[14,7,3],[1,14,8],[4,14,15],[9,0,7],[14,3,9],[1,14,12],[11,3,6],[14,13,5],[12,14,11],[14,3,2],[8,14,3],[10,5,14],[14,4,1],[14,9,3],[10,1,11],[5,14,10],[14,2,11],[5,14,8],[14,10,1],[15,0,14],[14,10,15],[10,4,14],[14,15,2],[14,6,0],[14,1,15],[8,7,14],[13,6,14],[2,11,14],[11,14,2],[14,8,7],[4,2,14],[14,4,2],[14,10,2],[14,6,3],[13,14,4],[7,14,15],[14,13,12],[14,10,2],[7,14,1],[12,8,14],[6,9,14],[13,5,14],[14,2,10],[3,14,11],[6,14,12],[14,15,7],[12,10,3],[14,13,15],[8,14,11],[0,14,8],[14,0,2],[14,9,7],[12,14,10],[3,14,13],[2,14,12],[4,10,14],[13,6,14],[14,13,4],[14,15,2],[14,2,15],[14,7,10],[12,14,15],[7,5,14],[9,15,4],[14,12,7],[14,13,15],[7,0,8],[14,5,10],[7,14,0],[14,9,7],[9,14,1],[6,14,15],[3,12,14],[14,12,3],[0,5,14],[14,13,10],[14,3,2],[11,14,5],[14,3,10],[3,14,2],[11,14,2],[14,0,6],[4,3,0],[9,14,5],[14,7,4],[2,9,14],[14,8,10],[14,1,8],[13,14,12],[14,5,11],[1,13,14],[6,14,9],[14,6,8],[3,14,11],[7,1,10],[2,8,14],[5,15,14],[5,15,14],[1,14,7],[11,14,12],[5,14,1],[14,13,9],[0,14,2],[14,11,4],[2,3,14],[11,10,13],[15,14,1],[14,15,11],[2,8,3],[14,0,9],[2,9,14],[7,14,1],[14,12,11],[14,12,2],[14,10,9],[14,7,5],[14,9,10],[9,14,0],[13,10,14],[14,7,10],[14,15,7],[14,10,15],[14,6,2],[8,2,6],[2,7,14],[14,11,5],[5,14,0],[0,3,14],[0,15,13],[1,6,0],[2,14,10],[14,1,10],[5,14,9],[12,14,9],[14,10,8],[8,2,9],[14,4,3],[14,3,11],[9,4,3],[14,5,4],[14,4,9],[8,1,11],[14,2,8],[0,14,13],[2,7,1],[14,1,9],[14,6,3],[1,13,14],[15,11,12],[0,2,1],[14,10,12],[3,10,14],[14,13,7],[14,0,11],[15,14,2],[4,14,8],[6,7,4],[12,7,14],[6,5,1],[14,9,12],[5,14,7],[7,14,10],[14,7,5],[14,5,0],[4,14,11],[4,3,8],[1,14,8],[11,14,6],[14,7,11],[10,14,7],[10,4,12],[14,8,11],[5,15,9],[14,15,11],[14,9,1],[9,11,8],[14,9,10],[13,14,4],[14,13,6],[13,14,0],[14,2,15]],[[2,12,14],[14,11,8],[0,14,15],[14,11,3],[14,2,15],[7,14,5],[14,3,4],[14,15,10],[0,6,14],[14,8,9],[6,14,4],[4,14,10],[1,5,13],[9,11,14],[9,3,2],[14,3,1],[9,5,14],[3,14,2],[7,5,14],[14,0,1],[12,1,9],[9,14,6],[12,10,5],[14,3,2],[3,14,11],[12,14,0],[4,14,0],[2,14,4],[6,0,2],[14,12,4],[9,14,7],[7,14,15],[14,9,5],[0,8,14],[3,14,7],[14,10,7],[1,14,4],[14,4,9],[14,0,12],[11,12,8],[9,14,1],[3,14,7],[10,14,11],[12,2,5],[14,3,10],[14,8,10],[10,6,14],[3,14,15],[3,12,1],[8,11,7],[14,13,6],[14,11,15],[14,11,3],[14,8,12],[14,11,6],[14,2,0],[10,1,14],[5,15,3],[14,11,6],[2,5,4],[8,15,14],[13,5,0],[14,9,13],[0,15,5],[9,7,6],[14,7,10],[14,4,10],[14,0,1],[14,12,9],[6,10,14],[14,3,10],[14,15,9],[11,14,8],[8,1,5],[14,6,9],[5,14,7],[15,14,12],[4,3,11],[10,14,5],[14,7,8],[15,1,9],[14,6,1],[0,14,13],[14,3,6],[14,4,6],[14,13,11],[14,1,10],[14,11,0],[14,0,10],[2,14,9],[14,0,2],[10,14,13],[11,5,10],[6,14,10],[14,10,13],[11,12,14],[12,14,2],[9,3,12],[14,1,7],[14,5,9],[7,6,8],[0,14,13],[10,14,6],[4,14,8],[14,2,8],[2,14,10],[14,11,7],[14,9,13],[13,10,14],[14,9,8],[6,14,13],[15,14,2],[6,7,12],[8,14,12],[14,0,9],[14,0,5],[6,5,14],[10,14,7],[14,10,15],[13,6,11],[14,11,2],[11,13,15],[15,14,2],[7,14,10],[9,1,4],[11,14,9],[3,12,14],[14,5,3],[3,5,14],[12,14,2],[14,12,1],[0,15,14],[5,13,12],[14,3,15],[9,13,11],[1,10,5],[0,14,1],[6,9,14],[7,14,1],[2,15,14],[14,9,11],[11,10,14],[8,15,4],[0,15,14],[14,9,15],[12,8,0],[3,7,11],[15,13,6],[9,7,15],[14,8,1],[14,6,10],[14,6,11],[13,14,4],[5,14,15],[14,9,2],[13,1,14],[14,6,15],[14,15,9],[14,0,12],[5,2,14],[14,13,11],[14,9,15],[14,13,8],[14,8,13],[12,10,8],[0,4,14],[6,14,15],[15,4,10],[11,14,2],[14,10,1],[14,5,10],[14,10,13],[15,7,14],[14,1,0],[1,7,10],[14,8,12],[6,1,7],[0,14,10],[10,12,0],[14,7,4],[14,12,9],[14,3,12],[3,4,14],[14,11,10],[14,4,2],[14,3,12],[4,14,11],[14,11,10],[14,10,6],[14,8,1],[14,3,2],[15,5,14],[15,9,14],[10,6,9],[7,13,0],[14,3,10],[10,14,3],[14,8,3],[1,14,2],[5,2,3],[12,13,14],[10,14,3],[5,12,14],[5,14,13],[14,4,7],[14,5,13],[14,0,4],[14,13,12],[7,9,14],[5,2,1],[5,14,4],[10,11,14],[12,14,15],[14,6,13],[12,9,14],[5,1,2],[14,8,11],[5,3,14],[12,9,14],[8,3,14],[14,7,6],[2,14,5],[14,7,12],[14,7,6],[11,14,0],[14,5,13],[6,10,14],[14,9,11],[6,14,11],[6,1,10],[3,6,14],[1,7,0],[14,6,1],[9,14,2],[9,8,10],[14,10,0],[6,14,0],[14,12,11],[8,14,1],[14,15,13],[14,3,0],[12,9,14],[13,14,3],[14,9,15],[14,6,12],[4,3,9],[14,2,11],[14,5,15],[6,14,5],[12,7,14],[14,6,9],[14,3,12],[7,0,14],[5,14,4],[14,0,5],[10,14,2],[14,13,9],[14,15,10],[7,8,14],[14,10,3],[14,7,2],[12,2,14],[14,11,1],[15,6,14],[15,14,3],[10,14,7],[14,7,8],[10,14,1],[14,12,2],[8,14,1],[14,13,3],[14,3,15],[14,7,12],[7,14,0],[4,14,3],[1,8,14],[14,10,8],[14,3,5],[14,15,2],[1,14,4],[0,9,14],[14,0,9],[3,14,1],[15,14,3],[11,14,8],[6,14,0],[5,15,14],[14,0,2],[6,7,14],[14,3,5],[5,14,1],[14,1,10],[14,8,1],[10,13,6],[6,1,9],[0,14,4],[7,14,12],[12,0,10],[14,1,11],[8,9,14],[14,0,12],[14,3,0],[14,2,5],[11,9,5],[14,15,6],[14,4,5],[8,2,3],[14,1,4],[14,11,10],[14,9,15],[14,10,5],[14,3,5],[4,15,14],[6,14,3],[14,2,4],[14,2,1],[14,11,10],[5,3,10],[14,1,9],[14,15,11],[14,13,11],[7,14,15],[14,2,12],[13,14,9],[14,11,13],[13,14,3],[9,14,11],[12,13,14],[12,13,3],[0,7,10],[8,14,15],[14,8,10],[14,3,13],[3,7,14],[0,14,10],[13,14,11],[14,0,8],[14,5,6],[1,13,9],[10,14,2],[14,7,13],[14,5,13],[7,10,2],[14,3,12],[14,2,6],[14,8,4],[2,14,6],[10,14,6],[15,14,7],[5,8,14],[11,14,1],[12,15,1],[14,10,0],[0,14,6],[10,15,7],[5,14,8],[10,8,6],[0,14,15],[4,12,6],[2,0,14],[13,5,14],[14,12,5],[14,15,13],[14,2,1],[10,1,14],[14,15,11],[14,3,5],[9,13,14],[14,8,6],[14,9,0],[14,6,9],[9,5,10],[8,3,14],[1,8,14],[0,14,9],[14,15,10],[12,13,4],[14,6,0],[14,9,0],[7,2,14],[8,14,0],[11,1,14],[3,15,14],[11,15,14],[0,11,14],[13,14,2],[14,9,2],[14,0,1],[15,14,6],[14,3,13],[8,13,14],[4,8,6],[14,3,2],[14,0,4],[14,1,2],[8,14,11],[14,13,2],[14,1,4],[2,14,7],[11,14,9],[15,0,14],[8,3,14],[14,1,7],[14,0,9],[0,13,5],[1,14,11],[6,14,15],[8,4,7],[15,14,8],[14,10,7],[14,10,8],[14,6,7],[2,0,8],[15,0,11],[5,2,14],[14,15,6],[14,2,0],[4,14,15],[14,15,3],[8,1,5],[14,1,11],[14,9,0],[14,9,8],[14,12,11],[14,5,11],[7,14,2],[14,13,9],[14,15,7],[3,4,6],[3,14,1],[14,15,0],[14,9,2],[14,12,6],[14,12,11],[14,6,3],[6,12,1],[7,14,0],[14,8,5],[14,15,3],[14,9,6],[1,8,14],[15,12,8],[10,15,4],[14,0,11],[14,3,1],[9,14,11],[4,10,14],[14,6,5],[14,10,7],[14,9,3],[11,14,4],[8,11,7],[4,5,14],[14,5,2],[14,3,12],[14,2,13],[14,3,10],[9,14,12],[6,13,9],[14,5,8],[14,1,9],[14,5,1],[11,14,12],[3,0,14],[14,9,1],[14,13,10],[14,8,1],[7,9,4],[5,7,8],[10,14,7],[11,3,4],[0,5,13],[14,9,12],[14,3,5],[14,4,9],[11,7,9],[13,14,15],[14,2,9],[13,14,7],[14,0,6],[7,14,13],[14,2,15],[10,14,1],[8,14,7],[14,10,4],[12,14,8],[14,3,15],[14,9,7],[13,14,9],[14,3,8],[14,9,15],[4,5,13],[5,1,7],[15,11,0],[10,14,12],[7,14,6],[14,0,8],[14,2,7],[4,6,3],[1,14,9],[14,8,2],[2,14,12],[14,4,1],[6,3,9],[3,14,5],[14,12,1],[14,4,1],[15,14,3],[14,3,1],[2,5,4],[14,13,15],[0,12,14]],[[8,3,7],[14,6,3],[6,14,8],[14,12,4],[14,13,3],[14,6,4],[14,7,11],[7,14,12],[0,14,5],[14,8,13],[14,13,11],[14,12,13],[14,11,10],[0,14,8],[7,9,4],[9,14,0],[2,9,14],[14,7,15],[14,6,0],[14,4,3],[6,14,12],[9,14,6],[9,14,2],[9,14,7],[7,0,14],[3,14,10],[14,0,10],[11,7,14],[5,14,7],[9,14,2],[15,1,14],[11,14,1],[14,12,2],[5,14,12],[5,14,6],[14,15,9],[1,0,13],[0,14,5],[14,13,6],[6,11,8],[0,14,1],[0,14,10],[4,14,7],[12,14,13],[14,9,2],[14,7,10],[0,14,2],[14,3,6],[9,12,10],[14,5,11],[14,5,4],[2,14,10],[14,10,7],[1,14,12],[14,10,3],[14,5,13],[9,14,12],[14,13,12],[14,6,15],[14,1,9],[14,5,2],[5,4,14],[9,14,15],[10,15,1],[14,12,5],[14,5,0],[14,12,13],[8,9,15],[14,9,1],[14,11,0],[1,11,14],[3,10,8],[14,6,0],[12,11,8],[1,14,11],[14,8,3],[3,13,7],[10,4,5],[12,4,11],[14,0,10],[6,8,14],[1,0,14],[14,15,9],[7,11,14],[7,2,14],[0,14,3],[14,0,4],[6,14,4],[14,11,13],[5,14,9],[14,11,12],[14,13,5],[4,13,14],[14,12,3],[0,8,5],[14,15,0],[2,1,14],[15,14,2],[14,1,4],[14,6,12],[11,2,6],[5,15,12],[11,3,2],[6,1,3],[3,15,14],[7,10,0],[11,3,2],[6,1,12],[4,14,8],[14,9,5],[12,14,7],[14,6,11],[14,0,13],[5,14,11],[3,14,12],[9,14,11],[14,5,8],[10,7,15],[3,14,10],[14,3,10],[14,6,10],[13,7,15],[5,14,3],[11,3,15],[14,13,12],[14,12,11],[14,8,4],[14,9,12],[8,14,12],[14,9,7],[8,2,14],[14,15,8],[8,14,9],[14,12,2],[0,5,6],[10,3,1],[3,9,14],[9,14,6],[14,11,15],[14,6,1],[14,2,4],[0,3,1],[14,8,10],[2,11,14],[14,9,13],[14,3,9],[5,15,14],[3,2,8],[14,13,15],[3,14,4],[11,13,4],[14,4,11],[11,14,7],[14,6,5],[14,6,1],[6,14,0],[14,3,0],[13,15,14],[14,8,1],[8,4,3],[4,14,5],[1,9,14],[14,6,3],[14,5,15],[0,14,9],[14,6,7],[3,6,14],[14,2,7],[14,11,9],[14,8,13],[14,2,13],[5,14,1],[12,14,1],[14,6,1],[14,3,7],[14,11,4],[8,9,14],[2,12,13],[3,14,10],[10,3,4],[12,14,5],[14,15,0],[11,14,7],[14,11,13],[10,15,14],[14,12,13],[10,15,14],[14,12,8],[14,15,7],[14,6,5],[5,14,15],[0,14,1],[14,7,12],[2,14,7],[14,8,4],[6,14,11],[6,14,1],[14,3,4],[3,14,2],[14,11,3],[2,0,14],[8,4,14],[8,4,3],[11,14,0],[13,4,8],[0,15,10],[14,15,9],[11,14,1],[14,0,7],[14,13,11],[14,4,3],[7,14,12],[14,10,11],[4,14,6],[14,3,11],[14,10,6],[12,7,14],[11,8,3],[15,14,6],[15,10,5],[14,4,1],[12,8,14],[14,9,6],[14,9,1],[13,5,8],[11,6,13],[14,8,2],[14,0,9],[14,7,8],[14,13,1],[14,0,10],[14,0,2],[14,11,9],[9,1,2],[14,12,3],[15,11,9],[1,14,15],[11,8,15],[14,9,1],[8,14,1],[14,12,2],[14,0,9],[14,1,12],[14,1,7],[4,6,14],[14,0,15],[6,14,5],[14,9,10],[8,13,6],[9,13,15],[10,14,13],[3,14,12],[8,9,14],[14,9,10],[14,15,8],[14,5,6],[7,5,9],[14,11,13],[4,15,14],[12,14,2],[3,10,14],[6,1,11],[14,0,13],[14,9,0],[14,5,11],[11,6,14],[10,14,8],[7,10,14],[14,13,15],[11,14,1],[14,7,15],[8,3,14],[14,13,7],[14,13,3],[3,11,7],[10,3,14],[14,13,3],[14,10,4],[14,10,11],[14,15,7],[7,10,14],[6,14,3],[14,7,6],[14,3,13],[14,9,5],[15,14,3],[14,10,3],[5,14,13],[14,12,13],[14,5,7],[8,5,4],[14,5,4],[7,14,15],[14,13,3],[14,9,7],[14,8,7],[14,2,5],[14,4,3],[9,3,2],[1,14,10],[11,14,7],[14,15,3],[7,14,13],[14,1,13],[11,14,9],[9,14,4],[11,14,13],[12,14,0],[3,14,5],[14,9,8],[6,5,0],[14,9,3],[0,5,2],[14,2,4],[14,9,5],[9,1,3],[7,14,8],[14,8,1],[6,5,3],[14,3,0],[2,10,9],[2,13,12],[8,4,0],[7,8,14],[8,1,6],[14,12,3],[14,15,3],[14,11,15],[4,9,14],[0,4,6],[5,14,13],[14,8,15],[0,1,4],[14,3,4],[6,3,8],[2,9,14],[14,3,9],[7,14,13],[14,7,6],[5,14,7],[5,14,2],[0,14,4],[6,10,13],[15,1,4],[14,12,13],[12,10,13],[14,12,5],[14,7,15],[8,15,14],[12,8,14],[3,14,8],[14,8,15],[14,15,4],[14,10,9],[4,10,12],[3,14,15],[11,6,14],[0,5,14],[8,14,4],[14,7,4],[11,14,7],[14,5,4],[8,6,11],[2,14,8],[14,15,5],[14,2,1],[6,9,14],[14,4,6],[12,11,14],[0,14,5],[10,1,8],[15,2,10],[14,7,11],[14,5,4],[14,13,9],[14,13,5],[7,12,3],[7,5,10],[14,6,8],[15,13,14],[14,9,5],[14,7,11],[14,10,8],[6,14,7],[14,15,13],[14,13,12],[14,3,12],[14,3,11],[9,14,4],[14,15,9],[8,2,14],[14,11,7],[14,8,9],[14,2,12],[2,3,12],[1,14,0],[1,14,9],[14,10,15],[4,12,13],[15,2,6],[14,2,0],[14,2,13],[15,0,5],[14,0,10],[15,14,13],[14,9,3],[14,9,15],[14,12,3],[6,14,2],[0,14,3],[1,5,4],[2,14,7],[7,14,9],[14,10,2],[1,14,5],[1,10,14],[14,13,4],[14,12,7],[14,1,15],[3,14,0],[14,9,10],[14,11,5],[8,0,14],[14,12,9],[14,9,2],[11,5,14],[4,14,5],[14,9,10],[8,15,14],[9,1,14],[1,13,5],[14,8,13],[14,2,9],[5,14,4],[14,10,6],[4,15,14],[2,14,0],[9,6,14],[14,8,5],[4,11,12],[15,4,14],[4,2,12],[0,9,14],[14,8,15],[14,15,0],[14,5,3],[10,2,14],[0,14,10],[14,6,15],[14,4,2],[14,2,4],[14,1,3],[14,11,0],[14,11,6],[14,13,4],[10,14,3],[14,15,6],[11,2,1],[1,12,9],[9,14,11],[15,13,0],[8,1,14],[0,14,10],[14,3,2],[11,2,13],[13,10,14],[8,14,7],[9,13,4],[14,11,6],[14,9,1],[13,0,12],[14,5,0],[10,4,11],[6,0,1],[14,11,8],[2,4,13],[7,6,14],[10,14,8],[14,6,10],[14,2,9],[14,11,8],[14,8,6],[14,1,10],[2,11,14],[0,5,9],[7,1,14],[14,5,8],[15,12,14],[15,11,9],[14,3,7],[6,9,14],[15,10,14],[6,14,9],[14,1,9],[14,0,15],[14,7,10],[2,11,7],[14,2,3],[12,10,9],[14,13,9],[14,1,5],[1,13,5],[10,14,9],[14,15,0],[12,1,6],[5,15,6],[0,12,10],[14,7,12],[4,12,0],[4,14,0],[14,11,13],[14,8,12]],[[14,7,0],[13,4,14],[14,0,4],[4,6,14],[14,4,0],[3,5,14],[14,4,8],[10,5,15],[9,1,10],[14,6,11],[9,3,14],[2,13,1],[14,12,5],[1,14,12],[2,14,6],[7,6,14],[3,4,14],[9,8,2],[2,4,10],[14,5,6],[11,14,10],[12,14,1],[14,10,5],[14,7,2],[14,2,1],[9,3,14],[4,3,14],[4,14,12],[14,2,11],[14,9,6],[6,14,13],[8,14,5],[14,13,4],[9,5,14],[14,10,4],[4,14,9],[4,14,9],[3,14,8],[11,7,14],[15,14,2],[14,10,5],[10,14,3],[4,14,8],[15,14,10],[14,1,13],[2,1,13],[12,14,10],[14,15,1],[14,9,0],[11,14,15],[15,8,14],[2,14,13],[0,2,1],[14,1,0],[14,15,13],[12,14,15],[1,11,14],[14,9,3],[14,4,2],[8,14,7],[14,2,7],[14,12,8],[14,4,7],[14,4,10],[14,3,4],[14,7,4],[14,12,2],[13,7,14],[4,14,0],[11,4,14],[14,5,10],[14,8,3],[14,15,7],[14,15,6],[5,1,6],[3,14,8],[14,4,10],[13,3,5],[0,14,8],[14,13,4],[14,4,9],[15,14,2],[14,13,5],[14,5,7],[7,14,13],[14,13,3],[4,8,14],[6,0,14],[11,14,1],[14,12,3],[8,4,5],[14,9,3],[14,15,0],[14,7,4],[12,2,14],[14,15,3],[6,14,8],[14,10,12],[14,10,1],[14,10,2],[4,2,14],[14,11,15],[7,15,4],[13,9,8],[13,14,2],[14,0,5],[14,4,6],[14,3,0],[14,0,9],[14,11,8],[13,2,14],[15,14,9],[1,14,13],[8,7,14],[3,11,14],[14,0,10],[10,9,12],[14,9,6],[15,14,4],[7,12,14],[8,14,15],[14,2,11],[14,2,13],[14,2,11],[14,3,15],[14,13,5],[7,10,14],[5,14,7],[14,5,9],[9,14,4],[10,15,14],[2,15,12],[6,9,13],[14,9,5],[11,7,14],[9,14,13],[1,0,2],[14,6,7],[10,11,4],[14,13,4],[14,4,12],[8,14,5],[8,14,11],[2,9,13],[14,0,5],[8,1,7],[14,15,4],[15,2,11],[6,7,14],[9,5,14],[8,15,10],[14,0,8],[7,5,1],[4,0,5],[1,14,11],[0,15,12],[14,9,7],[13,6,10],[1,14,11],[14,6,1],[10,14,9],[1,5,12],[3,14,7],[14,4,13],[11,4,14],[12,14,6],[13,14,10],[2,12,0],[14,4,2],[14,15,4],[14,1,4],[9,8,10],[8,10,14],[14,4,9],[14,8,1],[14,2,9],[14,11,15],[12,14,0],[11,14,2],[14,0,1],[14,13,10],[14,5,7],[14,6,10],[13,6,3],[7,15,14],[15,9,14],[12,5,4],[4,13,14],[13,14,15],[14,1,10],[14,11,4],[14,7,0],[14,15,11],[14,10,8],[4,10,14],[6,14,3],[14,8,2],[7,8,14],[13,12,4],[1,14,11],[14,5,12],[15,14,5],[8,12,14],[13,14,8],[14,10,5],[14,0,3],[12,14,3],[3,14,12],[14,6,9],[6,7,14],[14,12,6],[10,14,0],[14,3,9],[14,6,9],[9,1,10],[7,1,11],[8,11,3],[2,14,4],[4,14,9],[14,12,10],[5,11,15],[14,1,13],[14,8,6],[14,7,10],[14,3,2],[14,3,6],[0,10,14],[14,8,0],[8,14,3],[14,2,10],[7,14,13],[3,14,6],[7,12,14],[5,3,1],[14,4,0],[14,8,9],[4,14,15],[9,13,14],[13,2,5],[14,11,0],[9,14,4],[14,15,3],[2,14,8],[14,13,4],[7,14,15],[14,4,11],[4,14,2],[1,13,14],[4,1,11],[14,7,5],[13,14,0],[14,0,11],[14,4,0],[14,12,10],[12,8,14],[12,2,14],[10,11,14],[14,0,10],[14,8,0],[14,10,5],[4,10,14],[6,14,12],[12,14,8],[1,15,4],[13,14,3],[14,11,9],[3,6,14],[2,7,14],[0,4,9],[14,3,7],[3,10,1],[14,9,4],[10,14,3],[14,8,7],[6,10,14],[14,11,9],[14,15,9],[14,0,15],[0,4,2],[10,0,14],[14,10,8],[14,9,4],[1,8,11],[14,15,0],[10,14,6],[13,14,8],[0,9,4],[0,14,1],[14,1,6],[1,14,9],[14,2,11],[14,7,11],[14,11,9],[6,0,14],[14,12,6],[9,14,0],[7,10,1],[8,9,14],[6,4,14],[14,15,2],[3,14,1],[5,14,4],[14,13,4],[7,14,9],[14,4,2],[1,14,6],[3,6,14],[0,13,3],[14,3,4],[2,14,9],[0,10,14],[3,14,5],[11,0,14],[15,14,6],[0,15,13],[0,1,14],[14,9,15],[1,13,14],[2,14,0],[9,14,11],[1,8,14],[14,8,10],[6,14,2],[12,10,13],[14,6,9],[8,14,2],[2,15,9],[14,2,3],[2,6,14],[0,2,14],[5,0,10],[4,11,14],[0,14,12],[3,13,11],[0,14,6],[14,9,15],[15,14,13],[6,11,14],[14,8,15],[14,8,9],[14,2,12],[14,1,7],[14,9,3],[7,8,15],[14,9,7],[2,14,8],[5,14,15],[9,13,4],[4,13,8],[1,14,6],[14,12,10],[14,8,0],[11,14,12],[11,0,14],[7,9,3],[14,7,0],[8,13,4],[3,1,4],[14,5,15],[14,0,15],[3,2,14],[14,2,5],[14,5,8],[14,10,7],[14,3,6],[1,14,6],[9,15,14],[1,12,9],[5,7,12],[5,13,14],[3,14,7],[14,5,7],[12,14,9],[2,3,14],[11,13,14],[14,4,12],[3,1,14],[9,14,13],[15,7,6],[4,11,8],[14,1,2],[2,14,7],[12,14,4],[2,1,9],[10,14,15],[6,14,1],[14,6,15],[6,14,5],[13,5,14],[14,11,4],[12,14,15],[14,2,11],[1,14,3],[12,14,3],[6,2,8],[14,8,7],[14,11,10],[14,0,1],[14,9,6],[6,14,11],[7,4,14],[14,6,1],[14,4,9],[4,14,10],[4,12,14],[14,3,8],[14,9,3],[14,12,11],[6,8,7],[13,4,11],[12,11,14],[14,7,13],[1,14,9],[12,6,9],[11,0,14],[3,6,14],[9,5,4],[9,14,8],[11,14,6],[2,14,8],[14,3,10],[0,14,9],[5,2,14],[1,8,14],[14,0,10],[14,3,8],[8,5,12],[14,8,10],[9,14,12],[5,2,14],[14,6,12],[14,5,7],[8,5,14],[14,12,5],[10,7,14],[14,1,10],[14,9,2],[5,0,14],[14,12,13],[15,14,6],[4,1,3],[10,14,3],[0,5,7],[14,15,11],[5,14,12],[11,14,9],[14,2,12],[12,6,14],[0,14,9],[1,11,3],[14,8,15],[14,10,0],[13,14,11],[14,9,12],[14,4,9],[6,1,14],[14,13,2],[2,14,7],[3,14,12],[8,14,11],[14,12,11],[14,13,8],[13,14,10],[15,9,2],[3,7,14],[7,13,8],[14,13,10],[14,1,5],[14,8,15],[12,4,14],[14,8,1],[14,1,10],[10,14,9],[13,14,7],[7,14,6],[4,9,14],[14,4,13],[3,14,2],[1,14,11],[2,14,6],[14,1,11],[5,11,14],[8,1,14],[14,12,4],[14,2,6],[2,14,6],[13,14,4],[9,14,8],[14,15,3],[2,14,8],[14,11,10],[12,14,13],[14,9,10],[14,2,7],[14,15,0],[8,13,11],[1,15,0],[0,5,14],[14,5,8],[11,14,8],[8,13,7],[14,7,11],[14,7,10],[14,5,7],[6,14,10],[6,11,15],[13,2,1],[11,2,14],[14,1,5],[14,2,1],[15,14,0],[14,6,7]],[[7,8,14],[14,13,11],[14,12,13],[8,6,14],[14,15,12],[13,6,14],[13,14,3],[5,14,4],[0,1,14],[6,1,14],[14,9,11],[4,14,3],[14,4,8],[12,14,2],[14,4,15],[14,11,9],[14,3,11],[14,1,2],[12,7,14],[5,9,14],[14,12,3],[13,4,14],[1,0,7],[6,14,8],[8,14,7],[15,3,8],[3,5,14],[7,14,13],[0,10,14],[14,7,3],[6,11,14],[11,6,2],[4,14,2],[7,15,0],[13,14,15],[6,14,0],[14,12,0],[14,15,2],[14,15,9],[15,6,2],[14,2,10],[14,10,0],[8,12,14],[14,4,7],[9,6,15],[7,1,13],[5,13,2],[14,2,0],[11,14,9],[12,14,0],[14,11,10],[14,12,11],[0,14,11],[14,10,6],[8,14,6],[14,8,5],[14,2,7],[14,3,7],[2,14,10],[14,15,6],[12,0,3],[13,14,0],[14,12,15],[12,14,13],[6,14,12],[4,10,14],[6,13,14],[14,4,7],[14,4,7],[12,14,9],[15,14,12],[11,14,10],[9,7,5],[3,15,13],[5,14,7],[14,10,2],[14,9,15],[14,11,2],[14,3,8],[7,14,6],[12,0,11],[1,12,14],[1,5,14],[14,4,2],[4,9,6],[9,14,6],[9,6,8],[14,2,10],[14,12,1],[14,8,1],[14,0,10],[9,14,12],[5,1,14],[7,14,8],[14,4,11],[14,0,6],[14,8,1],[2,4,12],[14,4,2],[4,5,14],[10,12,14],[12,15,3],[9,14,10],[5,14,12],[3,14,8],[15,6,14],[0,9,13],[12,13,9],[4,12,14],[14,9,10],[14,3,13],[13,14,4],[8,14,7],[11,14,3],[10,14,11],[8,14,2],[6,11,15],[6,13,11],[14,8,2],[14,9,13],[11,2,15],[14,9,6],[14,6,8],[7,6,0],[7,14,5],[10,9,14],[14,13,7],[2,15,14],[6,14,13],[14,2,0],[14,9,7],[10,14,12],[0,14,2],[14,4,3],[14,9,4],[4,14,6],[15,0,14],[14,0,1],[7,14,10],[12,14,10],[10,14,2],[14,5,9],[11,14,6],[9,2,8],[14,6,4],[14,0,1],[11,8,5],[0,8,1],[2,10,14],[4,6,10],[14,15,3],[14,12,13],[6,8,14],[14,6,1],[1,14,9],[13,14,3],[14,9,5],[4,5,14],[3,10,2],[14,3,5],[9,14,2],[14,10,13],[8,14,5],[8,14,10],[1,7,4],[14,9,3],[13,15,11],[14,6,9],[13,14,0],[9,1,3],[14,9,15],[14,13,0],[14,2,7],[6,9,14],[0,14,4],[14,7,1],[12,14,8],[11,4,1],[14,1,13],[14,2,13],[7,9,3],[1,14,13],[13,1,12],[14,7,11],[14,5,0],[10,12,13],[11,14,13],[14,11,0],[14,11,13],[14,2,12],[0,14,2],[14,7,5],[5,14,12],[14,10,4],[9,14,13],[5,8,15],[13,5,6],[14,6,10],[14,3,6],[3,12,11],[14,11,4],[14,5,0],[15,14,11],[9,14,12],[14,7,1],[14,2,13],[14,12,9],[9,4,5],[12,14,5],[14,12,3],[1,14,12],[14,5,8],[1,6,14],[13,5,10],[14,7,15],[2,14,8],[14,9,15],[3,14,5],[14,9,5],[8,2,15],[14,11,1],[5,14,13],[13,15,0],[5,13,14],[1,14,13],[14,1,2],[15,6,4],[0,12,3],[14,11,10],[14,9,13],[0,9,4],[5,3,10],[10,2,0],[14,13,15],[6,0,11],[5,14,1],[14,12,10],[8,4,12],[2,5,14],[14,9,15],[14,11,1],[14,1,13],[14,7,10],[4,6,11],[14,9,0],[14,11,3],[1,3,5],[10,12,11],[6,14,11],[10,3,14],[2,14,13],[14,3,6],[4,14,10],[2,15,5],[14,11,4],[14,10,6],[1,14,15],[14,6,11],[10,6,14],[14,7,8],[10,14,4],[1,2,10],[8,9,2],[11,14,0],[14,11,5],[0,14,2],[14,13,11],[15,14,6],[13,14,10],[14,8,0],[14,10,0],[0,12,14],[14,15,10],[2,14,8],[3,11,14],[5,14,13],[3,14,10],[14,4,3],[0,6,14],[14,10,15],[3,13,14],[0,14,13],[1,0,13],[10,1,14],[14,5,13],[4,1,14],[12,7,14],[14,11,8],[14,4,7],[14,8,3],[14,10,13],[0,14,10],[14,15,12],[14,15,9],[10,14,5],[6,14,11],[0,14,13],[14,2,12],[12,14,6],[10,11,14],[4,0,11],[3,8,10],[14,10,8],[3,10,14],[14,4,6],[14,5,1],[14,10,8],[11,14,4],[14,8,5],[5,14,10],[10,14,12],[2,1,3],[14,6,0],[14,9,2],[4,14,10],[3,15,14],[14,0,6],[3,4,14],[14,10,8],[13,6,14],[14,12,8],[14,7,3],[0,1,3],[1,14,15],[4,14,3],[8,11,14],[14,4,3],[14,9,3],[1,14,8],[14,12,0],[6,9,15],[14,9,0],[6,14,2],[14,9,3],[14,5,15],[1,14,2],[14,13,7],[0,12,3],[14,12,2],[2,4,8],[2,8,14],[14,4,2],[8,1,14],[0,4,5],[0,8,15],[14,5,1],[10,11,14],[0,6,3],[10,13,14],[12,13,6],[14,9,12],[14,11,1],[0,9,15],[9,4,10],[14,5,10],[14,9,3],[14,0,10],[14,6,9],[7,14,2],[13,2,14],[14,1,15],[14,15,9],[11,14,13],[5,0,8],[9,14,13],[1,14,4],[14,6,1],[14,4,8],[1,12,14],[5,14,6],[0,14,8],[15,14,13],[11,14,4],[0,4,12],[14,13,7],[14,9,11],[14,3,15],[6,14,9],[3,8,14],[14,5,4],[4,14,0],[14,5,0],[14,7,12],[6,14,1],[14,5,8],[14,13,6],[14,10,7],[11,14,0],[14,7,5],[14,4,15],[7,5,14],[14,1,15],[3,6,14],[2,14,9],[14,9,1],[12,14,5],[4,15,0],[14,5,1],[14,10,6],[1,14,10],[14,11,15],[0,2,5],[10,9,14],[15,0,14],[14,15,9],[14,12,8],[14,0,9],[14,3,8],[14,9,7],[14,8,0],[14,7,13],[14,12,6],[14,10,0],[12,1,14],[3,15,2],[3,2,14],[15,6,11],[6,14,0],[14,11,6],[0,1,4],[4,7,14],[14,9,1],[7,11,14],[5,9,14],[4,12,10],[14,3,12],[9,14,15],[4,14,12],[14,8,5],[14,8,1],[7,12,10],[4,10,14],[14,0,10],[9,14,15],[14,12,4],[14,1,6],[4,14,9],[14,1,10],[9,11,1],[14,9,4],[10,14,7],[11,15,6],[14,0,3],[10,2,14],[14,1,13],[14,12,11],[10,13,2],[14,3,15],[1,14,12],[10,6,3],[14,12,8],[7,14,12],[9,1,4],[14,1,13],[14,4,5],[9,4,0],[11,1,13],[14,1,15],[5,7,14],[14,11,1],[3,14,10],[3,14,11],[15,14,10],[14,9,2],[14,9,11],[0,14,5],[14,12,13],[14,12,0],[3,14,4],[14,7,10],[3,7,14],[14,3,4],[9,14,3],[13,2,14],[14,7,4],[14,10,12],[14,11,8],[2,14,3],[14,7,5],[14,11,4],[14,9,3],[14,10,3],[14,12,3],[15,14,12],[8,6,14],[14,3,4],[14,4,12],[11,2,13],[13,5,6],[10,14,3],[13,8,5],[10,2,5],[14,11,15],[7,10,14],[14,13,4],[14,11,8],[14,13,15],[14,2,7],[11,7,10],[10,14,2],[14,12,13],[5,14,6],[11,1,14],[14,2,4],[14,15,6],[14,13,3],[5,9,4],[7,5,4],[4,3,14],[14,5,8],[0,14,4],[14,4,1]],[[8,14,6],[14,5,15],[14,15,2],[14,8,0],[14,5,3],[1,9,2],[12,14,11],[13,14,9],[9,14,0],[6,13,14],[7,1,15],[12,5,13],[14,0,11],[6,14,15],[8,4,3],[12,2,3],[13,14,7],[14,13,0],[8,9,14],[14,3,15],[14,1,0],[7,0,14],[3,14,10],[14,1,6],[14,2,8],[11,14,6],[1,14,0],[14,15,1],[13,15,14],[14,2,8],[3,0,8],[4,14,2],[7,13,14],[7,6,5],[2,0,14],[14,2,15],[14,2,13],[14,1,13],[14,6,13],[7,9,13],[8,6,10],[11,8,1],[14,4,8],[12,2,14],[14,3,11],[1,6,14],[9,14,5],[1,8,0],[2,14,11],[11,14,10],[15,5,14],[1,7,14],[4,14,8],[14,7,2],[15,13,2],[7,14,8],[14,11,9],[14,6,7],[14,2,1],[8,7,2],[14,12,15],[11,14,7],[13,11,9],[10,11,8],[14,9,6],[14,13,12],[14,6,4],[0,8,2],[11,10,12],[11,14,12],[10,14,12],[2,14,1],[14,6,3],[14,0,11],[4,9,14],[14,2,1],[11,14,0],[14,5,7],[11,13,14],[14,0,5],[13,5,7],[9,14,4],[7,4,14],[14,10,11],[14,12,2],[7,2,13],[14,1,13],[14,5,0],[13,14,12],[14,11,2],[14,2,9],[14,8,5],[14,10,5],[6,14,8],[3,14,6],[14,5,0],[14,2,10],[7,3,0],[14,13,11],[14,5,1],[0,14,11],[7,13,10],[14,11,8],[14,6,11],[14,2,7],[10,3,7],[14,7,9],[10,7,14],[14,13,8],[14,13,9],[11,14,8],[14,15,8],[1,8,14],[14,2,6],[3,14,9],[14,10,4],[12,14,10],[14,3,2],[14,0,4],[14,6,11],[12,10,4],[14,9,11],[15,14,10],[14,11,2],[14,7,9],[14,10,15],[12,15,14],[13,9,10],[14,13,8],[14,2,1],[2,14,9],[14,0,13],[6,4,14],[0,14,7],[6,14,3],[14,13,11],[1,14,9],[14,11,6],[10,14,12],[9,14,6],[13,1,14],[14,0,6],[2,14,3],[4,8,14],[14,2,15],[5,14,6],[1,11,2],[7,14,15],[2,14,11],[14,12,6],[4,13,14],[9,14,13],[14,6,3],[7,4,14],[11,14,13],[14,3,5],[15,11,14],[14,15,13],[0,14,2],[7,4,14],[9,6,15],[12,10,14],[14,7,12],[14,7,2],[14,4,1],[14,2,7],[12,2,8],[2,5,8],[14,3,2],[5,14,7],[9,2,12],[14,9,1],[14,3,6],[11,4,13],[14,11,8],[3,14,2],[0,14,12],[14,15,0],[14,0,6],[11,14,12],[14,5,10],[14,13,7],[8,14,6],[14,7,0],[14,4,1],[14,7,13],[10,14,5],[14,11,0],[12,4,1],[14,5,12],[5,4,6],[14,6,2],[14,11,3],[14,10,6],[14,11,1],[2,14,6],[12,2,1],[6,9,3],[12,0,8],[14,13,11],[14,13,8],[2,7,13],[14,4,10],[2,6,14],[5,0,11],[14,4,9],[14,12,1],[11,7,13],[15,14,6],[12,14,13],[13,14,7],[8,4,14],[4,14,0],[14,4,5],[8,7,14],[14,12,9],[2,9,14],[14,8,1],[14,12,15],[14,11,9],[11,10,9],[14,3,6],[14,3,9],[11,14,9],[14,0,5],[12,14,1],[0,14,1],[14,4,13],[1,15,5],[5,14,7],[14,10,9],[14,1,0],[14,11,5],[14,1,11],[7,14,1],[6,14,2],[10,12,14],[4,14,8],[10,14,4],[14,10,4],[14,7,15],[5,13,14],[4,14,9],[15,14,13],[11,14,15],[3,8,14],[14,4,0],[3,12,14],[8,14,15],[14,0,12],[14,15,8],[12,3,14],[14,11,10],[9,15,14],[9,14,1],[14,11,9],[2,10,8],[14,12,11],[8,7,3],[9,14,12],[6,14,13],[7,14,2],[14,10,15],[14,2,10],[15,14,13],[14,1,9],[9,5,14],[10,8,14],[15,8,14],[2,14,0],[4,15,14],[14,4,3],[14,8,6],[8,14,0],[14,11,4],[5,15,14],[14,4,15],[14,10,1],[14,2,8],[3,14,0],[14,9,15],[14,6,8],[3,2,14],[0,5,11],[14,7,13],[11,5,6],[14,15,1],[14,13,6],[0,13,3],[15,14,10],[13,14,8],[14,15,2],[14,3,0],[11,14,4],[9,14,13],[0,8,14],[12,14,3],[11,4,14],[4,14,12],[14,9,12],[14,1,10],[8,3,5],[4,6,1],[14,0,3],[0,14,12],[14,8,7],[14,13,11],[14,8,5],[14,6,3],[14,13,11],[12,13,14],[14,15,13],[12,2,5],[14,0,9],[14,4,15],[3,11,14],[5,7,0],[14,5,3],[14,5,0],[15,0,6],[14,15,8],[14,8,15],[8,14,10],[14,3,11],[15,14,2],[4,11,14],[12,14,1],[13,7,14],[14,2,8],[3,8,9],[14,15,13],[14,2,8],[14,4,1],[14,4,1],[5,3,14],[14,3,0],[6,3,14],[3,13,14],[4,2,9],[2,8,11],[7,14,11],[14,12,9],[3,14,8],[14,7,2],[0,14,13],[9,14,8],[14,6,12],[14,12,7],[14,11,10],[2,14,8],[7,1,14],[8,2,14],[2,14,13],[11,14,2],[14,7,5],[6,5,14],[4,14,10],[14,3,7],[14,13,2],[5,4,13],[14,0,4],[14,7,11],[3,11,14],[8,7,13],[11,0,14],[14,8,2],[2,0,6],[14,7,12],[8,7,12],[15,14,7],[14,7,9],[11,14,10],[12,10,1],[14,4,1],[13,11,6],[14,4,9],[0,14,11],[6,10,12],[9,14,0],[10,14,9],[8,14,1],[14,11,12],[9,14,8],[14,7,1],[4,5,7],[10,14,5],[1,2,5],[15,14,10],[15,5,3],[14,12,4],[8,14,13],[7,14,1],[14,5,8],[2,7,14],[14,2,10],[14,8,10],[15,14,1],[14,2,3],[6,14,11],[12,14,5],[14,4,15],[11,14,1],[3,2,13],[9,14,2],[10,5,9],[3,2,14],[8,14,6],[2,15,5],[12,9,2],[8,14,13],[14,4,3],[12,9,6],[0,1,14],[14,7,12],[14,2,8],[3,14,10],[0,14,12],[10,2,14],[15,11,10],[6,14,5],[14,15,9],[13,5,6],[14,0,3],[14,9,3],[6,10,15],[3,14,9],[4,2,14],[2,13,14],[2,14,5],[14,15,0],[3,13,1],[14,13,0],[15,14,7],[13,14,1],[10,3,6],[14,11,7],[14,7,3],[10,6,8],[14,12,7],[14,10,8],[15,7,1],[3,11,9],[2,14,4],[14,9,3],[14,11,4],[1,8,14],[5,14,4],[14,12,4],[14,4,0],[10,14,4],[14,10,6],[8,14,1],[7,14,2],[14,11,10],[9,5,14],[1,6,14],[7,9,14],[11,14,15],[1,2,14],[14,1,15],[14,0,10],[14,11,15],[8,3,14],[14,15,3],[15,14,5],[0,14,9],[14,3,6],[14,7,6],[8,5,7],[14,2,13],[14,15,1],[14,13,5],[14,2,9],[14,2,1],[3,1,8],[5,9,1],[14,6,9],[14,4,0],[14,1,9],[14,3,15],[9,14,0],[8,15,7],[2,14,5],[15,0,5],[14,3,5],[14,7,8],[9,5,14],[10,14,13],[14,2,7],[14,6,11],[14,15,5],[15,7,5],[14,10,6],[14,9,11],[14,5,0],[6,14,12],[14,7,11],[2,3,1],[10,14,7],[8,14,5],[13,1,0],[13,9,15],[14,2,9],[14,4,5],[14,9,4],[6,10,14],[5,12,10],[6,14,7],[5,1,14],[14,8,3],[14,4,5],[14,15,11]],[[2,14,6],[14,11,8],[8,14,12],[14,12,7],[4,1,8],[8,14,9],[9,8,14],[13,11,14],[15,5,13],[14,1,9],[14,3,8],[14,9,11],[5,14,3],[11,6,14],[14,8,4],[9,7,14],[14,9,3],[14,15,1],[11,14,13],[0,8,14],[13,15,9],[14,5,11],[14,1,11],[14,8,15],[14,9,4],[1,15,14],[15,14,10],[8,13,2],[14,10,5],[14,9,12],[14,13,1],[13,14,10],[13,14,1],[14,1,15],[3,14,12],[14,3,2],[14,13,1],[14,2,6],[1,15,10],[5,14,9],[14,11,0],[12,9,0],[14,11,6],[14,7,6],[7,14,8],[14,9,13],[7,2,14],[12,14,4],[14,6,1],[14,11,9],[13,14,9],[14,0,1],[14,10,13],[14,11,4],[1,14,13],[9,3,14],[11,14,10],[6,14,1],[12,2,0],[2,14,12],[14,13,4],[1,14,3],[1,15,14],[11,14,12],[14,13,0],[14,13,4],[7,14,11],[7,14,2],[14,10,8],[3,14,9],[14,10,15],[11,14,2],[11,10,14],[14,2,6],[14,0,15],[15,14,1],[15,14,0],[8,3,11],[14,0,8],[7,14,12],[6,15,8],[15,14,4],[8,1,15],[8,2,12],[14,0,1],[7,14,9],[13,2,14],[8,14,3],[14,0,3],[6,14,12],[13,14,2],[4,14,3],[0,1,14],[0,14,2],[14,10,6],[1,3,15],[7,14,4],[14,6,0],[3,14,0],[14,5,3],[14,5,12],[14,11,7],[4,7,14],[12,3,14],[14,11,10],[14,12,0],[14,11,12],[10,9,8],[15,14,4],[2,13,10],[14,15,5],[14,8,13],[9,15,8],[14,3,6],[15,2,14],[14,5,13],[14,15,5],[14,0,1],[6,13,14],[14,2,8],[5,14,1],[8,14,2],[12,14,13],[4,14,2],[14,7,9],[7,13,8],[5,7,12],[9,4,10],[2,15,14],[10,4,8],[12,14,0],[11,14,15],[9,14,6],[2,11,6],[10,14,8],[4,3,10],[14,12,15],[1,5,14],[14,8,1],[12,0,15],[6,8,9],[14,11,8],[14,0,1],[2,15,14],[15,0,7],[10,13,9],[12,5,7],[1,14,0],[9,14,2],[14,9,12],[14,1,7],[11,14,0],[13,7,10],[14,5,0],[14,8,12],[7,9,3],[15,14,9],[14,9,6],[14,8,6],[14,3,13],[14,0,2],[5,7,14],[11,14,12],[0,4,15],[0,15,4],[14,9,3],[5,14,3],[9,2,6],[14,8,6],[1,9,6],[14,1,5],[9,1,0],[7,14,0],[14,15,0],[14,15,9],[14,15,6],[14,5,9],[5,2,14],[3,14,5],[5,12,14],[12,14,1],[14,12,2],[12,9,8],[14,2,15],[8,12,14],[14,12,13],[14,2,4],[3,14,6],[14,9,15],[14,0,12],[7,2,14],[7,14,4],[14,2,9],[13,3,14],[14,0,7],[14,7,9],[13,14,2],[5,14,8],[3,7,2],[13,14,8],[7,14,13],[11,9,14],[14,0,7],[14,15,1],[14,10,8],[1,14,10],[14,0,10],[11,14,5],[14,15,5],[14,4,9],[14,5,7],[14,13,6],[15,14,13],[14,0,15],[2,6,7],[6,12,14],[14,8,3],[6,3,14],[5,2,12],[7,14,9],[14,10,4],[14,3,12],[6,5,14],[9,5,14],[10,9,11],[5,14,10],[14,13,7],[1,3,14],[8,11,15],[5,0,13],[14,13,1],[14,6,8],[14,13,1],[4,14,11],[14,9,8],[3,14,6],[14,15,0],[14,1,4],[14,2,13],[3,5,14],[14,9,6],[14,6,2],[10,15,7],[2,14,3],[1,3,14],[14,13,0],[1,14,12],[4,14,3],[14,3,6],[14,3,4],[14,13,3],[8,14,4],[14,4,15],[14,5,4],[11,14,13],[14,2,13],[3,14,7],[6,14,5],[14,6,7],[6,11,4],[14,13,8],[2,4,14],[14,10,4],[10,14,2],[1,0,6],[5,14,4],[0,15,14],[6,9,7],[0,14,5],[14,0,15],[14,11,15],[13,14,1],[14,6,11],[1,14,3],[13,0,14],[4,12,14],[14,7,8],[3,1,14],[14,11,1],[14,10,4],[6,1,14],[14,10,12],[14,8,3],[14,1,5],[9,4,15],[14,12,9],[14,12,3],[2,9,15],[14,5,2],[5,14,12],[2,14,1],[14,13,8],[7,14,4],[0,11,14],[11,15,14],[15,8,12],[14,13,12],[14,11,15],[9,14,10],[5,14,13],[0,14,13],[2,13,6],[15,14,2],[14,12,8],[11,14,6],[10,6,8],[1,14,0],[8,2,14],[15,7,14],[14,4,11],[6,14,4],[8,7,14],[2,14,6],[8,6,1],[7,14,12],[14,1,4],[5,7,12],[14,6,1],[11,8,14],[14,11,4],[9,14,7],[3,14,7],[14,5,4],[14,3,5],[10,0,14],[3,14,2],[14,9,0],[12,14,5],[14,9,1],[14,15,9],[14,3,10],[1,14,11],[7,14,10],[6,1,14],[5,14,13],[7,14,1],[6,14,8],[14,0,3],[15,14,0],[14,13,1],[11,2,14],[1,0,3],[11,14,4],[11,3,4],[5,14,4],[9,15,14],[14,4,3],[15,14,8],[0,2,14],[14,5,0],[8,11,14],[14,1,3],[14,3,11],[14,7,12],[14,1,5],[14,1,10],[3,12,14],[8,14,10],[12,14,3],[14,3,1],[14,12,15],[12,0,7],[14,0,8],[6,14,2],[3,14,0],[4,14,12],[9,8,14],[8,1,9],[2,9,5],[14,11,10],[14,0,10],[10,1,7],[5,14,7],[14,12,2],[14,13,9],[14,11,4],[1,6,7],[11,12,14],[14,12,10],[4,6,14],[2,1,0],[14,15,6],[6,14,13],[5,6,11],[14,2,10],[14,4,1],[14,1,4],[7,14,6],[14,0,13],[14,15,6],[5,14,7],[1,14,3],[14,7,3],[14,13,7],[0,14,7],[15,14,8],[14,15,0],[14,2,3],[13,14,2],[7,3,14],[1,6,2],[3,1,9],[14,5,4],[10,14,8],[14,8,6],[13,8,0],[14,1,0],[7,14,9],[0,14,1],[14,6,4],[5,10,3],[14,10,15],[0,3,14],[1,14,2],[8,9,14],[14,3,10],[14,2,6],[14,13,0],[1,4,12],[14,1,8],[14,13,7],[14,9,13],[14,1,3],[11,14,15],[14,10,2],[14,6,5],[11,14,3],[14,7,12],[14,5,10],[8,14,1],[1,14,9],[15,14,5],[4,14,6],[9,13,14],[1,13,14],[8,14,3],[11,14,6],[4,14,7],[4,11,2],[1,14,8],[0,14,10],[14,4,3],[10,14,1],[14,6,8],[14,2,5],[14,5,7],[2,15,11],[14,3,0],[14,3,11],[5,15,7],[8,14,4],[14,9,1],[14,7,8],[8,14,10],[14,13,6],[14,3,11],[14,5,7],[7,10,14],[14,3,4],[8,14,4],[9,12,14],[10,14,5],[14,15,4],[14,3,6],[13,14,1],[14,8,10],[14,8,5],[10,5,6],[14,6,3],[9,14,3],[4,12,15],[12,14,8],[14,5,9],[2,4,3],[1,5,15],[6,14,12],[2,7,1],[14,1,13],[0,1,14],[5,14,1],[14,4,1],[14,10,8],[12,14,15],[7,14,11],[1,9,14],[14,3,9],[14,1,6],[10,4,5],[6,14,0],[4,14,9],[9,14,4],[13,5,14],[14,9,15],[14,6,2],[5,12,4],[7,14,13],[14,1,7],[8,7,14],[14,4,5],[4,0,6],[14,8,12],[14,12,0],[9,3,2],[14,15,10],[4,8,7],[6,8,14],[14,15,1],[0,7,14],[5,14,10],[14,15,4],[0,14,2],[3,14,12]],[[13,5,14],[14,8,15],[14,0,4],[15,1,14],[15,6,4],[6,14,9],[14,11,13],[14,7,8],[14,7,15],[4,3,14],[14,2,0],[9,3,5],[14,5,0],[14,6,11],[9,15,14],[14,3,5],[12,4,0],[14,15,9],[14,11,2],[12,14,1],[12,13,3],[15,14,4],[14,2,9],[12,13,3],[14,11,0],[14,0,7],[10,8,3],[14,10,8],[14,7,8],[14,13,9],[12,7,14],[14,7,0],[14,7,2],[8,10,5],[2,14,13],[15,0,14],[14,8,9],[2,1,14],[11,14,6],[6,14,13],[13,12,14],[0,14,9],[14,2,7],[7,3,10],[14,1,7],[3,2,14],[11,9,14],[14,5,4],[10,14,11],[2,14,12],[12,14,8],[11,14,1],[14,9,15],[10,15,3],[14,7,1],[14,12,1],[3,4,7],[14,10,5],[6,14,12],[14,6,10],[14,1,4],[14,7,11],[14,13,2],[14,13,3],[5,11,6],[4,15,14],[0,13,14],[6,10,14],[2,3,14],[0,6,3],[3,14,10],[14,8,1],[14,9,15],[14,3,10],[9,3,15],[8,14,3],[3,14,6],[14,1,13],[14,8,1],[1,14,3],[14,10,9],[14,0,7],[14,1,3],[4,14,0],[0,14,7],[10,14,4],[14,6,0],[8,10,1],[3,2,15],[11,15,14],[15,14,7],[14,9,2],[6,14,3],[1,7,9],[14,4,9],[10,14,1],[12,6,14],[2,4,8],[15,13,1],[11,5,14],[7,14,3],[3,14,9],[13,14,6],[14,10,0],[2,8,13],[10,14,3],[14,0,3],[9,10,6],[4,14,15],[5,0,14],[0,14,10],[7,14,4],[14,2,11],[10,6,7],[10,4,14],[14,7,8],[12,14,8],[11,15,10],[4,14,5],[8,5,14],[9,6,13],[14,6,9],[14,15,7],[14,1,11],[14,2,9],[7,4,5],[3,14,10],[0,14,4],[6,15,14],[0,2,14],[14,15,5],[5,3,6],[9,6,14],[4,14,10],[7,0,14],[8,1,7],[3,5,14],[6,14,15],[7,14,8],[14,2,13],[14,6,3],[0,10,14],[7,14,2],[14,7,8],[10,14,0],[14,12,1],[14,2,0],[14,1,6],[14,12,2],[7,1,14],[2,3,14],[1,14,7],[14,12,3],[11,1,3],[14,12,13],[14,4,9],[14,9,12],[14,0,3],[13,7,9],[12,14,8],[14,15,5],[14,6,1],[14,0,1],[10,14,7],[0,9,15],[5,13,14],[4,12,14],[0,14,5],[14,0,11],[14,11,10],[15,13,14],[1,14,10],[14,10,11],[13,12,14],[3,14,13],[1,6,14],[7,11,3],[9,11,1],[7,3,14],[14,15,2],[14,0,10],[0,8,13],[14,12,4],[14,9,2],[14,8,11],[14,0,9],[14,10,3],[10,9,12],[14,2,8],[14,7,8],[4,10,14],[14,11,3],[14,10,12],[13,4,6],[15,13,8],[14,0,12],[3,2,6],[2,14,12],[4,14,5],[12,5,14],[4,5,12],[15,12,8],[11,8,4],[8,14,2],[12,14,0],[14,6,2],[2,10,14],[2,13,14],[12,15,14],[14,4,6],[14,15,11],[13,1,14],[6,13,1],[14,2,15],[14,1,2],[13,14,12],[14,3,4],[3,4,10],[14,4,3],[11,14,3],[14,10,5],[8,14,11],[4,14,0],[3,8,7],[14,12,9],[14,6,13],[14,12,3],[1,14,11],[10,14,8],[14,2,11],[12,14,8],[14,8,6],[14,15,10],[14,10,12],[1,14,13],[5,14,7],[0,14,6],[14,3,2],[14,13,0],[9,7,14],[13,8,2],[0,14,3],[5,10,8],[3,2,0],[2,13,9],[14,9,12],[14,15,8],[15,2,13],[15,0,10],[7,14,1],[11,0,12],[14,11,13],[14,6,13],[4,14,15],[10,14,3],[14,15,4],[14,4,10],[13,14,15],[15,14,3],[15,9,14],[3,7,14],[5,3,7],[14,2,15],[5,9,14],[1,14,12],[0,10,7],[14,12,13],[4,10,8],[14,12,7],[14,3,1],[14,5,11],[5,13,3],[14,10,7],[10,7,14],[0,14,7],[0,14,3],[14,3,13],[14,1,9],[6,14,4],[6,14,13],[2,8,13],[14,12,9],[14,2,9],[14,12,10],[7,14,8],[14,12,6],[14,10,13],[11,14,3],[14,2,0],[5,14,11],[14,7,0],[14,13,1],[9,12,14],[3,7,9],[6,14,0],[4,14,15],[7,4,12],[12,11,15],[14,5,2],[14,2,3],[14,1,3],[0,14,15],[10,1,14],[14,15,5],[8,14,15],[14,6,10],[15,3,0],[11,14,12],[12,3,2],[14,8,4],[14,0,13],[14,7,11],[3,4,5],[14,10,11],[14,9,8],[6,14,1],[11,4,10],[14,6,4],[14,2,6],[0,7,14],[10,14,12],[14,8,5],[14,2,9],[9,6,12],[10,14,6],[14,3,10],[14,9,11],[14,12,13],[14,7,10],[13,14,11],[2,13,15],[7,14,9],[5,14,2],[2,9,14],[13,14,12],[12,14,8],[3,14,9],[15,5,1],[14,6,3],[2,14,13],[10,3,13],[14,3,13],[14,12,5],[4,13,0],[0,15,6],[10,11,6],[6,11,4],[0,14,6],[7,0,14],[0,10,14],[15,14,1],[14,6,11],[12,10,14],[7,6,12],[6,14,3],[14,7,15],[2,4,14],[3,14,2],[14,15,13],[14,0,2],[11,14,2],[14,12,7],[8,14,6],[12,10,14],[12,14,6],[15,9,14],[14,1,7],[8,14,12],[1,14,11],[14,8,4],[14,15,5],[14,15,1],[12,4,14],[10,14,6],[11,12,2],[0,14,8],[14,3,9],[8,14,0],[14,7,5],[14,11,8],[14,11,15],[11,14,10],[14,7,5],[14,10,5],[14,4,6],[14,7,9],[14,1,8],[1,15,13],[1,14,7],[8,14,1],[1,14,4],[14,9,2],[4,7,0],[14,7,1],[14,3,13],[14,3,13],[13,8,4],[7,15,14],[8,14,1],[14,3,12],[4,14,1],[5,14,10],[14,7,4],[3,13,10],[14,1,10],[3,14,4],[3,14,12],[8,4,14],[14,3,11],[14,1,4],[14,8,0],[6,14,1],[14,8,12],[14,4,0],[14,15,11],[14,11,2],[14,0,12],[14,10,4],[14,1,12],[12,9,4],[3,2,14],[8,10,14],[3,13,9],[14,9,4],[2,15,12],[14,11,10],[8,14,3],[14,0,13],[14,7,3],[13,7,14],[5,14,4],[0,4,7],[14,13,5],[14,9,1],[2,4,14],[14,6,7],[6,12,14],[11,8,14],[14,6,9],[1,9,0],[14,3,6],[6,14,9],[9,15,14],[15,14,13],[14,2,5],[6,14,9],[14,15,11],[0,3,4],[14,12,3],[12,8,14],[13,2,7],[14,4,2],[14,8,1],[14,9,1],[14,6,2],[12,10,8],[14,7,10],[2,12,14],[14,6,5],[2,4,14],[14,15,12],[11,14,6],[14,6,2],[14,10,13],[14,9,8],[14,0,11],[3,6,14],[11,14,8],[14,2,12],[10,13,15],[3,14,5],[9,7,12],[4,14,11],[14,9,15],[2,14,7],[14,5,15],[10,14,5],[14,1,5],[14,1,8],[4,5,8],[7,9,5],[11,4,7],[15,14,7],[7,14,11],[4,14,8],[14,6,8],[1,14,12],[14,3,9],[15,4,12],[14,2,13],[1,2,6],[14,9,12],[11,1,14],[4,1,9],[14,11,3],[14,12,13],[0,14,12],[10,4,14],[5,3,4],[14,9,2],[14,7,8],[6,1,14],[13,10,14],[3,14,6],[10,4,6],[9,2,6],[6,14,9],[14,15,13],[12,10,4],[12,10,1],[14,8,12],[5,12,14]]]
CAP = 1491
YW = 1491
def setup_inputs(rng):
    return {"x": rng.standard_normal((N, 128, T), dtype=np.float32)}
def reference(x):
    y = np.full((N, 128, YW), np.nan, x.dtype)
    fill = [0] * N
    for r in range(N):
        for t in range(T):
            for e in ROUTE[r][t]:
                if fill[e] < CAP:
                    y[e][:, fill[e]] = x[r][:, t]
                fill[e] += 1
    return {"y": y}

@@ -1,0 +1,334 @@
+SCRATCH = {
+    "xs": ("sbuf", [128, 512], "float32"),
+    "pk": ("sbuf", [128, 624], "float32"),
+    "ld": ("sbuf", [128, 660], "float32"),
+    "gp": ("sbuf", [128, 740], "float32"),
+    "yi": ("sbuf", [128, 1491], "float32"),
+}
+SEMAPHORES = [
+    "lx",
+    "hx",
+    "ph", "lh",
+    "r0", "r1",
+    "k0", "k1",
+    "dg",
+    "a0", "a1", "a2",
+    "arr",
+    "sent",
+    "st",
+]
+
+HELP = (4, 6, 5, 7)
+CUT = 5
+G, SY, SC = 0, 1, 2
+
+_CACHE = {}
+
+
+def _runs(vals):
+    out = []
+    for k, v in enumerate(vals):
+        if out and out[-1][1] + out[-1][2] == v:
+            out[-1][2] += 1
+        else:
+            out.append([k, v, 1])
+    return out
+
+
+def _spread(n, k):
+    out, acc = [], 0
+    for _ in range(n):
+        acc += k
+        out.append(acc >= n)
+        if acc >= n:
+            acc -= n
+    return out
+
+
+def _ways(dest, n, nt):
+    cls = [dict() for _ in range(4)]
+    sets = [[None] * nt for _ in range(n)]
+    for r in range(n):
+        for t in range(nt):
+            s = tuple(sorted(set((e // 4 - r // 4) % 4 for e, _ in dest[r][t]) - {0}))
+            sets[r][t] = s
+            cls[r // 4].setdefault(s, []).append((r, t))
+
+    def num(h, s):
+        return len(cls[h].get(s, ()))
+
+    def cabled(h, d):
+        return h // 2 != ((h + d) % 4) // 2
+
+    tri = [3 if cabled((h + 1) % 4, 1) else 1 for h in range(4)]
+
+    def cost(v):
+        ed = dict(((h, d), 0) for h in range(4) for d in (1, 3))
+        for h in range(4):
+            a, x12, x23 = v[h], v[4 + h], v[8 + h]
+            y = num(h, (1, 2, 3)) if tri[h] == 1 else 0
+            both = num(h, (1, 3)) + num(h, (1, 2, 3))
+            ed[(h, 1)] += num(h, (1,)) + num(h, (1, 2)) + both + a + x23
+            ed[(h, 3)] += num(h, (3,)) + num(h, (2, 3)) + both + num(h, (2,)) - a + x12
+            ed[((h + 1) % 4, 1)] += a + x23 + num(h, (1, 2)) - x12 + y
+            ed[((h + 3) % 4, 3)] += num(h, (2,)) - a + x12 + num(h, (2, 3)) - x23 + num(h, (1, 2, 3)) - y
+        cab = [ed[k] for k in ed if cabled(*k)]
+        swi = [ed[k] for k in ed if not cabled(*k)]
+        rack = [sum(ed[k] for k in ed if cabled(*k) and k[0] // 2 == a) for a in (0, 1)]
+        out = [ed[(h, 1)] + ed[(h, 3)] for h in range(4)]
+        inn = [ed[((h + 3) % 4, 1)] + ed[((h + 1) % 4, 3)] for h in range(4)]
+        return 8 * max(rack) + 2 * max(cab) + max(swi) + max(out) + max(inn) + 1e-6 * sum(x * x for x in ed.values())
+
+    top = [num(h, (2,)) for h in range(4)] + [num(h, (1, 2)) for h in range(4)] + [num(h, (2, 3)) for h in range(4)]
+    v = [u // 2 for u in top[:4]] + [0] * 8
+    cur = cost(v)
+    for step in (64, 16, 4, 1):
+        moved = True
+        while moved:
+            moved = False
+            for i in range(12):
+                for s in (step, -step):
+                    w = list(v)
+                    w[i] = min(top[i], max(0, w[i] + s))
+                    c = cost(w)
+                    if c < cur - 1e-9:
+                        v, cur, moved = w, c, True
+    via = [[0] * nt for _ in range(n)]
+    for h in range(4):
+        for s, k1 in (((2,), v[h]), ((1, 2), num(h, (1, 2)) - v[4 + h]), ((2, 3), v[8 + h]),
+                      ((1, 2, 3), num(h, (1, 2, 3)) if tri[h] == 1 else 0)):
+            lst = cls[h].get(s, [])
+            for (r, t), f in zip(lst, _spread(len(lst), k1)):
+                via[r][t] = 1 if f else 3
+    return sets, via
+
+
+def _land(i, p):
+    return i if p == 0 else HELP[i]
+
+
+def _thresholds(edge, cut, nt):
+    thr = {}
+    for h in range(4):
+        for d in (1, 3):
+            load = [0.0] * 4
+            for i in range(4):
+                for t in edge[(4 * ((h - d) % 4) + i, d)][1]:
+                    load[_land(i, 0 if t < cut else 1) // 2] += 1
+                load[i // 2] += len(edge[(4 * h + i, d)][0]) + len(edge[(4 * h + i, d)][1])
+            share = [0.0] * 4
+            for _ in range(60):
+                for i in range(4):
+                    a, b = i // 2, HELP[i] // 2
+                    mv = (load[a] - load[b]) / 2
+                    mv = max(-share[i], min(len(edge[(4 * h + i, d)][0]) - share[i], mv))
+                    share[i] += mv
+                    load[a] -= mv
+                    load[b] += mv
+            for i in range(4):
+                k = edge[(4 * h + i, d)][0]
+                m = int(round(share[i]))
+                thr[(4 * h + i, d)] = k[len(k) - m] if m > 0 else nt
+    return thr
+
+
+def _emit(dest, cnt, edge, thr, cut, sl, nt, wc):
+    n = len(dest)
+    total = {}
+    used = {}
+    col = {}
+    msgs = {}
+    fwds = {}
+
+    def land(core, r, toks):
+        o = used.get(core, 0)
+        used[core] = o + len(toks)
+        for j, t in enumerate(toks):
+            col[(core, r, t)] = o + j
+        return o
+
+    for r in range(n):
+        h, i = r // 4, r % 4
+        for d in (1, 3):
+            side = 0 if d == 1 else 1
+            for p in (0, 1):
+                k, on = [[t for t in x if (t < cut) == (p == 0)] for x in edge[(r, d)]]
+                kr = [t for t in k if t < thr[(r, d)]]
+                kh = [t for t in k if t >= thr[(r, d)]]
+                lnd = wc((h + d) % 4, _land(i, p))
+                if kr or on:
+                    o = land(lnd, r, kr + on)
+                    msgs.setdefault(wc(h, i), []).append((lnd, o, kr + on, "r%d" % side))
+                if on:
+                    nxt = wc((h + 2) % 4, _land(i, p))
+                    fwds.setdefault(lnd, {})[side] = (nxt, land(nxt, r, on), o + len(kr), len(on))
+                if kh:
+                    msgs.setdefault(wc(h, HELP[i]), []).append((lnd, land(lnd, r, kh), kh, "k%d" % side))
+
+    prog = {}
+    size = {"pk": 0, "gp": 0, "ld": max(used.values())}
+    for h in range(4):
+        for c in range(8):
+            me = wc(h, c)
+            q = prog[me] = ([], [], [])
+            turn = [0]
+            mine = {}
+
+            def cp(dst, dc, src, sc, m, sem):
+                turn[0] ^= 1
+                q[SY if turn[0] else SC].append(("cp", dst, dc, src, sc, m, sem))
+                mine[sem] = mine.get(sem, 0) + 16
+
+            def done(sem):
+                if sem in mine:
+                    q[G].append(("w", sem, mine[sem]))
+
+            def send(to, dst, dc, src, sc, m, sem):
+                eng = 16 if to // 8 == me // 8 else 8
+                q[G].append(("rd", to, dst, dc, src, sc, m, sem))
+                total[(to, sem)] = total.get((to, sem), 0) + eng
+                total[(me, "sent")] = total.get((me, "sent"), 0) + eng
+
+            i = c if c < 4 else HELP.index(c)
+            r = 4 * h + i
+            lo = min(thr[(r, 1)], thr[(r, 3)], sl[r])
+            if c < 4:
+                q[SY].append(("ldx", "lx"))
+                for k in (G, SY, SC):
+                    q[k].append(("w", "lx", 16))
+                if lo < nt:
+                    send(wc(h, HELP[i]), "xs", lo, "xs", lo, nt - lo, "hx")
+            else:
+                for k in (G, SY, SC):
+                    q[k].append(("W", "hx"))
+            o = 0
+            outs = []
+            for (lnd, lcol, toks, sem) in msgs.get(me, []):
+                for (k0, t0, m) in _runs(toks):
+                    cp("pk", o + k0, "xs", t0, m, "ph")
+                outs.append((lnd, "ld", lcol, "pk", o, len(toks), sem))
+                o += len(toks)
+            near = []
+            for j in range(4):
+                lst = [(t, yc) for t in (range(0, sl[r]) if c < 4 else range(sl[r], nt))
+                       for (e, yc) in dest[r][t] if e == 4 * h + j]
+                for (k0, t0, m) in _runs([t for t, _ in lst]):
+                    if j == c:
+                        cp("yi", lst[0][1] + k0, "xs", t0, m, "lh")
+                    else:
+                        cp("pk", o + k0, "xs", t0, m, "lh")
+                if lst and j != c:
+                    near.append((wc(h, j), "yi", lst[0][1], "pk", o, len(lst), "arr"))
+                    o += len(lst)
+            size["pk"] = max(size["pk"], o)
+            done("ph")
+            for a in outs:
+                send(*a)
+            done("lh")
+            for a in near:
+                send(*a)
+            for side in (0, 1):
+                if side in fwds.get(me, {}):
+                    nxt, o2, o1, m = fwds[me][side]
+                    q[G].append(("W", "r%d" % side))
+                    send(nxt, "ld", o2, "ld", o1, m, "dg")
+            o = 0
+            for u, (hs, sems) in enumerate((((h + 3) % 4, ("r0", "k0")), ((h + 1) % 4, ("r1", "k1")),
+                                            ((h + 2) % 4, ("dg",)))):
+                s = 4 * hs + i
+                for k in (G, SY, SC):
+                    for sem in sems:
+                        q[k].append(("W", sem))
+                outs = []
+                for j in range(4):
+                    lst = [(col[(me, s, t)], yc) for t in (range(0, cut) if c < 4 else range(cut, nt))
+                           for (e, yc) in dest[s][t] if e == 4 * h + j]
+                    for (k0, c0, m) in _runs([a for a, _ in lst]):
+                        if j == c:
+                            cp("yi", lst[0][1] + k0, "ld", c0, m, "a%d" % u)
+                        else:
+                            cp("gp", o + k0, "ld", c0, m, "a%d" % u)
+                    if lst and j != c:
+                        outs.append((wc(h, j), "yi", lst[0][1], "gp", o, len(lst), "arr"))
+                        o += len(lst)
+                done("a%d" % u)
+                for a in outs:
+                    send(*a)
+            size["gp"] = max(size["gp"], o)
+            if c < 4:
+                q[G].append(("W", "arr"))
+                q[G].append(("sty", cnt[r], "st"))
+                q[G].append(("w", "st", 16))
+            q[G].append(("W", "sent"))
+    for me in prog:
+        prog[me] = [[(("w", op[1], total[(me, op[1])]) if op[0] == "W" else op)
+                     for op in ql if op[0] != "W" or (me, op[1]) in total] for ql in prog[me]]
+    return prog, size
+
+
+def _plan(tables, cores):
+    route, cap, nt = tables["ROUTE"], tables["CAP"], tables["T"]
+    n = len(route)
+    chip0 = [cores[4 * h] - cores[4 * h] % 8 for h in range(4)]
+
+    def wc(h, c):
+        return chip0[h] + c
+
+    fill = [0] * n
+    dest = [[None] * nt for _ in range(n)]
+    for r in range(n):
+        for t in range(nt):
+            dest[r][t] = [(e, fill[e]) for e in route[r][t] if fill[e] < cap]
+            for e in route[r][t]:
+                fill[e] += 1
+    cnt = [min(f, cap) for f in fill]
+    sets, via = _ways(dest, n, nt)
+    edge = {}
+    for r in range(n):
+        for d in (1, 3):
+            on = [2 in sets[r][t] and via[r][t] == d for t in range(nt)]
+            edge[(r, d)] = ([t for t in range(nt) if d in sets[r][t] and not on[t]], [t for t in range(nt) if on[t]])
+    cut = nt * CUT // 16
+    thr = _thresholds(edge, cut, nt)
+    prog, _ = _emit(dest, cnt, edge, thr, cut, [nt] * n, nt, wc)
+    sl = []
+    for r in range(n):
+        h, i = r // 4, r % 4
+        a, b = [sum(1 for ql in prog[wc(h, c)] for op in ql if op[0] == "cp" and op[6] != "lh") for c in (i, HELP[i])]
+        here = [set(e for e, _ in dest[r][t] if e // 4 == h) for t in range(nt)] + [set()]
+        start = [len(here[t] - here[t - 1]) for t in range(nt)]
+        best = None
+        for s in range(nt, -1, -1):
+            w = max(a + sum(start[:s]), b + sum(start[s:]) + len(here[s] & here[s - 1]))
+            if best is None or w < best[0]:
+                best = (w, s)
+        sl.append(best[1])
+    prog, size = _emit(dest, cnt, edge, thr, cut, sl, nt, wc)
+    for k, v in size.items():
+        assert v <= SCRATCH[k][1][1], (k, v)
+    return prog, size
+
+
+def rank_program(g, core, T, topo):
+    if "plan" not in _CACHE:
+        _CACHE["plan"] = _plan(T.tables, T.cores)[0]
+    queues = _CACHE["plan"].get(core)
+    if queues is None:
+        return
+    S = T.sem
+    for eng, ql in zip((g, g.sync, g.scalar), queues):
+        for op in ql:
+            if op[0] == "cp":
+                _, dst, dc, src, sc, m, sem = op
+                eng.dma_start(T[dst][:, dc:dc + m], T[src][:, sc:sc + m]).then_inc(S[sem], 16)
+            elif op[0] == "w":
+                eng.wait_ge(S[op[1]], op[2])
+            elif op[0] == "rd":
+                _, to, dst, dc, src, sc, m, sem = op
+                rid, pid = topo.addr(to, core)
+                eng.remote_dma(T[dst][:, dc:dc + m], T[src][:, sc:sc + m], S[sem], S.sent, pid, rid,
+                               topo.mask(core, to))
+            elif op[0] == "ldx":
+                eng.dma_start(T.xs[:], T.x[:]).then_inc(S[op[1]], 16)
+            elif op[0] == "sty":
+                eng.dma_start(T.y[:, 0:op[1]], T.yi[:, 0:op[1]]).then_inc(S[op[2]], 16)

@@ -1,8 +1,8 @@
 SCRATCH = {
     "xs": ("sbuf", [128, 512], "float32"),
-    "pk": ("sbuf", [128, 624], "float32"),
-    "ld": ("sbuf", [128, 660], "float32"),
-    "gp": ("sbuf", [128, 740], "float32"),
+    "pk": ("sbuf", [128, 601], "float32"),
+    "ld": ("sbuf", [128, 400], "float32"),
+    "gp": ("sbuf", [128, 449], "float32"),
     "yi": ("sbuf", [128, 1491], "float32"),
 }
 SEMAPHORES = [
@@ -17,8 +17,15 @@ SEMAPHORES = [
     "sent",
     "st",
 ]
+SEMS = {"sw": ("r0", "k0", "a0"), "cb": ("r1", "k1", "a1"), "dg": ("dg", "dg", "a2")}
 
-HELP = (4, 6, 5, 7)
+HELP = (4, 5, 6, 7)
+LAND = {
+    (0, "cb"): (0, 4), (0, "sw"): (16, 20), (0, "dg"): (21, 17),
+    (1, "cb"): (1, 5), (1, "sw"): (22, 18), (1, "dg"): (19, 23),
+    (2, "cb"): (2, 6), (2, "sw"): (10, 14), (2, "dg"): (10, 14),
+    (3, "cb"): (3, 7), (3, "sw"): (15, 11), (3, "dg"): (15, 11),
+}
 CUT = 5
 G, SY, SC = 0, 1, 2
 
@@ -45,6 +52,14 @@ def _spread(n, k):
     return out
 
 
+def _cabled(h, d):
+    return h // 2 != ((h + d) % 4) // 2
+
+
+def _rel(h, d):
+    return "cb" if _cabled(h, d) else "sw"
+
+
 def _ways(dest, n, nt):
     cls = [dict() for _ in range(4)]
     sets = [[None] * nt for _ in range(n)]
@@ -57,10 +72,7 @@ def _ways(dest, n, nt):
     def num(h, s):
         return len(cls[h].get(s, ()))
 
-    def cabled(h, d):
-        return h // 2 != ((h + d) % 4) // 2
-
-    tri = [3 if cabled((h + 1) % 4, 1) else 1 for h in range(4)]
+    tri = [3 if _cabled((h + 1) % 4, 1) else 1 for h in range(4)]
 
     def cost(v):
         ed = dict(((h, d), 0) for h in range(4) for d in (1, 3))
@@ -72,9 +84,9 @@ def _ways(dest, n, nt):
             ed[(h, 3)] += num(h, (3,)) + num(h, (2, 3)) + both + num(h, (2,)) - a + x12
             ed[((h + 1) % 4, 1)] += a + x23 + num(h, (1, 2)) - x12 + y
             ed[((h + 3) % 4, 3)] += num(h, (2,)) - a + x12 + num(h, (2, 3)) - x23 + num(h, (1, 2, 3)) - y
-        cab = [ed[k] for k in ed if cabled(*k)]
-        swi = [ed[k] for k in ed if not cabled(*k)]
-        rack = [sum(ed[k] for k in ed if cabled(*k) and k[0] // 2 == a) for a in (0, 1)]
+        cab = [ed[k] for k in ed if _cabled(*k)]
+        swi = [ed[k] for k in ed if not _cabled(*k)]
+        rack = [sum(ed[k] for k in ed if _cabled(*k) and k[0] // 2 == a) for a in (0, 1)]
         out = [ed[(h, 1)] + ed[(h, 3)] for h in range(4)]
         inn = [ed[((h + 3) % 4, 1)] + ed[((h + 1) % 4, 3)] for h in range(4)]
         return 8 * max(rack) + 2 * max(cab) + max(swi) + max(out) + max(inn) + 1e-6 * sum(x * x for x in ed.values())
@@ -103,18 +115,17 @@ def _ways(dest, n, nt):
     return sets, via
 
 
-def _land(i, p):
-    return i if p == 0 else HELP[i]
-
-
 def _thresholds(edge, cut, nt):
     thr = {}
     for h in range(4):
         for d in (1, 3):
             load = [0.0] * 4
+            back = (h - d) % 4
             for i in range(4):
-                for t in edge[(4 * ((h - d) % 4) + i, d)][1]:
-                    load[_land(i, 0 if t < cut else 1) // 2] += 1
+                for t in edge[(4 * back + i, d)][1]:
+                    c = LAND[(i, _rel(back, d))][0 if t < cut else 1]
+                    if c < 8:
+                        load[c // 2] += 1
                 load[i // 2] += len(edge[(4 * h + i, d)][0]) + len(edge[(4 * h + i, d)][1])
             share = [0.0] * 4
             for _ in range(60):
@@ -139,6 +150,7 @@ def _emit(dest, cnt, edge, thr, cut, sl, nt, wc):
     col = {}
     msgs = {}
     fwds = {}
+    units = {}
 
     def land(core, r, toks):
         o = used.get(core, 0)
@@ -149,27 +161,31 @@ def _emit(dest, cnt, edge, thr, cut, sl, nt, wc):
 
     for r in range(n):
         h, i = r // 4, r % 4
-        for d in (1, 3):
-            side = 0 if d == 1 else 1
-            for p in (0, 1):
+        for p in (0, 1):
+            far = wc((h + 2) % 4, LAND[(i, "dg")][p])
+            units.setdefault(far, {})["dg"] = (r, p)
+            for d in (1, 3):
+                rel = _rel(h, d)
                 k, on = [[t for t in x if (t < cut) == (p == 0)] for x in edge[(r, d)]]
                 kr = [t for t in k if t < thr[(r, d)]]
                 kh = [t for t in k if t >= thr[(r, d)]]
-                lnd = wc((h + d) % 4, _land(i, p))
+                lnd = wc((h + d) % 4, LAND[(i, rel)][p])
+                units.setdefault(lnd, {})[rel] = (r, p)
                 if kr or on:
                     o = land(lnd, r, kr + on)
-                    msgs.setdefault(wc(h, i), []).append((lnd, o, kr + on, "r%d" % side))
+                    msgs.setdefault(wc(h, i), []).append((lnd, o, kr + on, SEMS[rel][0]))
                 if on:
-                    nxt = wc((h + 2) % 4, _land(i, p))
-                    fwds.setdefault(lnd, {})[side] = (nxt, land(nxt, r, on), o + len(kr), len(on))
+                    fwds.setdefault(lnd, {})[rel] = (far, land(far, r, on), o + len(kr), len(on))
                 if kh:
-                    msgs.setdefault(wc(h, HELP[i]), []).append((lnd, land(lnd, r, kh), kh, "k%d" % side))
+                    msgs.setdefault(wc(h, HELP[i]), []).append((lnd, land(lnd, r, kh), kh, SEMS[rel][1]))
 
     prog = {}
     size = {"pk": 0, "gp": 0, "ld": max(used.values())}
     for h in range(4):
-        for c in range(8):
+        for c in range(24):
             me = wc(h, c)
+            if c >= 8 and me not in units:
+                continue
             q = prog[me] = ([], [], [])
             turn = [0]
             mine = {}
@@ -189,75 +205,77 @@ def _emit(dest, cnt, edge, thr, cut, sl, nt, wc):
                 total[(to, sem)] = total.get((to, sem), 0) + eng
                 total[(me, "sent")] = total.get((me, "sent"), 0) + eng
 
-            i = c if c < 4 else HELP.index(c)
-            r = 4 * h + i
-            lo = min(thr[(r, 1)], thr[(r, 3)], sl[r])
-            if c < 4:
-                q[SY].append(("ldx", "lx"))
-                for k in (G, SY, SC):
-                    q[k].append(("w", "lx", 16))
-                if lo < nt:
-                    send(wc(h, HELP[i]), "xs", lo, "xs", lo, nt - lo, "hx")
-            else:
-                for k in (G, SY, SC):
-                    q[k].append(("W", "hx"))
+            if c < 8:
+                i = c if c < 4 else HELP.index(c)
+                r = 4 * h + i
+                lo = min(thr[(r, 1)], thr[(r, 3)], sl[r])
+                if c < 4:
+                    q[SY].append(("ldx", "lx"))
+                    for k in (G, SY, SC):
+                        q[k].append(("w", "lx", 16))
+                    if lo < nt:
+                        send(wc(h, HELP[i]), "xs", lo, "xs", lo, nt - lo, "hx")
+                else:
+                    for k in (G, SY, SC):
+                        q[k].append(("W", "hx"))
+                o = 0
+                outs = []
+                for (lnd, lcol, toks, sem) in msgs.get(me, []):
+                    for (k0, t0, m) in _runs(toks):
+                        cp("pk", o + k0, "xs", t0, m, "ph")
+                    outs.append((lnd, "ld", lcol, "pk", o, len(toks), sem))
+                    o += len(toks)
+                near = []
+                for j in range(4):
+                    lst = [(t, yc) for t in (range(0, sl[r]) if c < 4 else range(sl[r], nt))
+                           for (e, yc) in dest[r][t] if e == 4 * h + j]
+                    for (k0, t0, m) in _runs([t for t, _ in lst]):
+                        if j == c:
+                            cp("yi", lst[0][1] + k0, "xs", t0, m, "lh")
+                        else:
+                            cp("pk", o + k0, "xs", t0, m, "lh")
+                    if lst and j != c:
+                        near.append((wc(h, j), "yi", lst[0][1], "pk", o, len(lst), "arr"))
+                        o += len(lst)
+                size["pk"] = max(size["pk"], o)
+                done("ph")
+                for a in outs:
+                    send(*a)
+                done("lh")
+                for a in near:
+                    send(*a)
+            for rel in ("sw", "cb"):
+                if rel in fwds.get(me, {}):
+                    far, o2, o1, m = fwds[me][rel]
+                    q[G].append(("W", SEMS[rel][0]))
+                    send(far, "ld", o2, "ld", o1, m, "dg")
             o = 0
-            outs = []
-            for (lnd, lcol, toks, sem) in msgs.get(me, []):
-                for (k0, t0, m) in _runs(toks):
-                    cp("pk", o + k0, "xs", t0, m, "ph")
-                outs.append((lnd, "ld", lcol, "pk", o, len(toks), sem))
-                o += len(toks)
-            near = []
-            for j in range(4):
-                lst = [(t, yc) for t in (range(0, sl[r]) if c < 4 else range(sl[r], nt))
-                       for (e, yc) in dest[r][t] if e == 4 * h + j]
-                for (k0, t0, m) in _runs([t for t, _ in lst]):
-                    if j == c:
-                        cp("yi", lst[0][1] + k0, "xs", t0, m, "lh")
-                    else:
-                        cp("pk", o + k0, "xs", t0, m, "lh")
-                if lst and j != c:
-                    near.append((wc(h, j), "yi", lst[0][1], "pk", o, len(lst), "arr"))
-                    o += len(lst)
-            size["pk"] = max(size["pk"], o)
-            done("ph")
-            for a in outs:
-                send(*a)
-            done("lh")
-            for a in near:
-                send(*a)
-            for side in (0, 1):
-                if side in fwds.get(me, {}):
-                    nxt, o2, o1, m = fwds[me][side]
-                    q[G].append(("W", "r%d" % side))
-                    send(nxt, "ld", o2, "ld", o1, m, "dg")
-            o = 0
-            for u, (hs, sems) in enumerate((((h + 3) % 4, ("r0", "k0")), ((h + 1) % 4, ("r1", "k1")),
-                                            ((h + 2) % 4, ("dg",)))):
-                s = 4 * hs + i
+            for rel in ("sw", "cb", "dg"):
+                if rel not in units.get(me, {}):
+                    continue
+                s, p = units[me][rel]
                 for k in (G, SY, SC):
-                    for sem in sems:
+                    for sem in sorted(set(SEMS[rel][:2])):
                         q[k].append(("W", sem))
                 outs = []
                 for j in range(4):
-                    lst = [(col[(me, s, t)], yc) for t in (range(0, cut) if c < 4 else range(cut, nt))
+                    lst = [(col[(me, s, t)], yc) for t in (range(0, cut) if p == 0 else range(cut, nt))
                            for (e, yc) in dest[s][t] if e == 4 * h + j]
                     for (k0, c0, m) in _runs([a for a, _ in lst]):
                         if j == c:
-                            cp("yi", lst[0][1] + k0, "ld", c0, m, "a%d" % u)
+                            cp("yi", lst[0][1] + k0, "ld", c0, m, SEMS[rel][2])
                         else:
-                            cp("gp", o + k0, "ld", c0, m, "a%d" % u)
+                            cp("gp", o + k0, "ld", c0, m, SEMS[rel][2])
                     if lst and j != c:
                         outs.append((wc(h, j), "yi", lst[0][1], "gp", o, len(lst), "arr"))
                         o += len(lst)
-                done("a%d" % u)
+                done(SEMS[rel][2])
                 for a in outs:
                     send(*a)
             size["gp"] = max(size["gp"], o)
             if c < 4:
                 q[G].append(("W", "arr"))
-                q[G].append(("sty", cnt[r], "st"))
+                q[G].append(("sty", cnt[4 * h + c], "st"))
                 q[G].append(("w", "st", 16))
             q[G].append(("W", "sent"))
     for me in prog:

SCRATCH = {
    "xs": ("sbuf", [128, 512], "float32"),
    "pk": ("sbuf", [128, 601], "float32"),
    "ld": ("sbuf", [128, 400], "float32"),
    "gp": ("sbuf", [128, 449], "float32"),
    "yi": ("sbuf", [128, 1491], "float32"),
}
SEMAPHORES = [
    "lx",
    "hx",
    "ph", "lh",
    "r0", "r1",
    "k0", "k1",
    "dg",
    "a0", "a1", "a2",
    "arr",
    "sent",
    "st",
]
SEMS = {"sw": ("r0", "k0", "a0"), "cb": ("r1", "k1", "a1"), "dg": ("dg", "dg", "a2")}

HELP = (4, 5, 6, 7)
LAND = {
    (0, "cb"): (0, 4), (0, "sw"): (16, 20), (0, "dg"): (21, 17),
    (1, "cb"): (1, 5), (1, "sw"): (22, 18), (1, "dg"): (19, 23),
    (2, "cb"): (2, 6), (2, "sw"): (10, 14), (2, "dg"): (10, 14),
    (3, "cb"): (3, 7), (3, "sw"): (15, 11), (3, "dg"): (15, 11),
}
CUT = 5
G, SY, SC = 0, 1, 2

_CACHE = {}


def _runs(vals):
    out = []
    for k, v in enumerate(vals):
        if out and out[-1][1] + out[-1][2] == v:
            out[-1][2] += 1
        else:
            out.append([k, v, 1])
    return out


def _spread(n, k):
    out, acc = [], 0
    for _ in range(n):
        acc += k
        out.append(acc >= n)
        if acc >= n:
            acc -= n
    return out


def _cabled(h, d):
    return h // 2 != ((h + d) % 4) // 2


def _rel(h, d):
    return "cb" if _cabled(h, d) else "sw"


def _ways(dest, n, nt):
    cls = [dict() for _ in range(4)]
    sets = [[None] * nt for _ in range(n)]
    for r in range(n):
        for t in range(nt):
            s = tuple(sorted(set((e // 4 - r // 4) % 4 for e, _ in dest[r][t]) - {0}))
            sets[r][t] = s
            cls[r // 4].setdefault(s, []).append((r, t))

    def num(h, s):
        return len(cls[h].get(s, ()))

    tri = [3 if _cabled((h + 1) % 4, 1) else 1 for h in range(4)]

    def cost(v):
        ed = dict(((h, d), 0) for h in range(4) for d in (1, 3))
        for h in range(4):
            a, x12, x23 = v[h], v[4 + h], v[8 + h]
            y = num(h, (1, 2, 3)) if tri[h] == 1 else 0
            both = num(h, (1, 3)) + num(h, (1, 2, 3))
            ed[(h, 1)] += num(h, (1,)) + num(h, (1, 2)) + both + a + x23
            ed[(h, 3)] += num(h, (3,)) + num(h, (2, 3)) + both + num(h, (2,)) - a + x12
            ed[((h + 1) % 4, 1)] += a + x23 + num(h, (1, 2)) - x12 + y
            ed[((h + 3) % 4, 3)] += num(h, (2,)) - a + x12 + num(h, (2, 3)) - x23 + num(h, (1, 2, 3)) - y
        cab = [ed[k] for k in ed if _cabled(*k)]
        swi = [ed[k] for k in ed if not _cabled(*k)]
        rack = [sum(ed[k] for k in ed if _cabled(*k) and k[0] // 2 == a) for a in (0, 1)]
        out = [ed[(h, 1)] + ed[(h, 3)] for h in range(4)]
        inn = [ed[((h + 3) % 4, 1)] + ed[((h + 1) % 4, 3)] for h in range(4)]
        return 8 * max(rack) + 2 * max(cab) + max(swi) + max(out) + max(inn) + 1e-6 * sum(x * x for x in ed.values())

    top = [num(h, (2,)) for h in range(4)] + [num(h, (1, 2)) for h in range(4)] + [num(h, (2, 3)) for h in range(4)]
    v = [u // 2 for u in top[:4]] + [0] * 8
    cur = cost(v)
    for step in (64, 16, 4, 1):
        moved = True
        while moved:
            moved = False
            for i in range(12):
                for s in (step, -step):
                    w = list(v)
                    w[i] = min(top[i], max(0, w[i] + s))
                    c = cost(w)
                    if c < cur - 1e-9:
                        v, cur, moved = w, c, True
    via = [[0] * nt for _ in range(n)]
    for h in range(4):
        for s, k1 in (((2,), v[h]), ((1, 2), num(h, (1, 2)) - v[4 + h]), ((2, 3), v[8 + h]),
                      ((1, 2, 3), num(h, (1, 2, 3)) if tri[h] == 1 else 0)):
            lst = cls[h].get(s, [])
            for (r, t), f in zip(lst, _spread(len(lst), k1)):
                via[r][t] = 1 if f else 3
    return sets, via


def _thresholds(edge, cut, nt):
    thr = {}
    for h in range(4):
        for d in (1, 3):
            load = [0.0] * 4
            back = (h - d) % 4
            for i in range(4):
                for t in edge[(4 * back + i, d)][1]:
                    c = LAND[(i, _rel(back, d))][0 if t < cut else 1]
                    if c < 8:
                        load[c // 2] += 1
                load[i // 2] += len(edge[(4 * h + i, d)][0]) + len(edge[(4 * h + i, d)][1])
            share = [0.0] * 4
            for _ in range(60):
                for i in range(4):
                    a, b = i // 2, HELP[i] // 2
                    mv = (load[a] - load[b]) / 2
                    mv = max(-share[i], min(len(edge[(4 * h + i, d)][0]) - share[i], mv))
                    share[i] += mv
                    load[a] -= mv
                    load[b] += mv
            for i in range(4):
                k = edge[(4 * h + i, d)][0]
                m = int(round(share[i]))
                thr[(4 * h + i, d)] = k[len(k) - m] if m > 0 else nt
    return thr


def _emit(dest, cnt, edge, thr, cut, sl, nt, wc):
    n = len(dest)
    total = {}
    used = {}
    col = {}
    msgs = {}
    fwds = {}
    units = {}

    def land(core, r, toks):
        o = used.get(core, 0)
        used[core] = o + len(toks)
        for j, t in enumerate(toks):
            col[(core, r, t)] = o + j
        return o

    for r in range(n):
        h, i = r // 4, r % 4
        for p in (0, 1):
            far = wc((h + 2) % 4, LAND[(i, "dg")][p])
            units.setdefault(far, {})["dg"] = (r, p)
            for d in (1, 3):
                rel = _rel(h, d)
                k, on = [[t for t in x if (t < cut) == (p == 0)] for x in edge[(r, d)]]
                kr = [t for t in k if t < thr[(r, d)]]
                kh = [t for t in k if t >= thr[(r, d)]]
                lnd = wc((h + d) % 4, LAND[(i, rel)][p])
                units.setdefault(lnd, {})[rel] = (r, p)
                if kr or on:
                    o = land(lnd, r, kr + on)
                    msgs.setdefault(wc(h, i), []).append((lnd, o, kr + on, SEMS[rel][0]))
                if on:
                    fwds.setdefault(lnd, {})[rel] = (far, land(far, r, on), o + len(kr), len(on))
                if kh:
                    msgs.setdefault(wc(h, HELP[i]), []).append((lnd, land(lnd, r, kh), kh, SEMS[rel][1]))

    prog = {}
    size = {"pk": 0, "gp": 0, "ld": max(used.values())}
    for h in range(4):
        for c in range(24):
            me = wc(h, c)
            if c >= 8 and me not in units:
                continue
            q = prog[me] = ([], [], [])
            turn = [0]
            mine = {}

            def cp(dst, dc, src, sc, m, sem):
                turn[0] ^= 1
                q[SY if turn[0] else SC].append(("cp", dst, dc, src, sc, m, sem))
                mine[sem] = mine.get(sem, 0) + 16

            def done(sem):
                if sem in mine:
                    q[G].append(("w", sem, mine[sem]))

            def send(to, dst, dc, src, sc, m, sem):
                eng = 16 if to // 8 == me // 8 else 8
                q[G].append(("rd", to, dst, dc, src, sc, m, sem))
                total[(to, sem)] = total.get((to, sem), 0) + eng
                total[(me, "sent")] = total.get((me, "sent"), 0) + eng

            if c < 8:
                i = c if c < 4 else HELP.index(c)
                r = 4 * h + i
                lo = min(thr[(r, 1)], thr[(r, 3)], sl[r])
                if c < 4:
                    q[SY].append(("ldx", "lx"))
                    for k in (G, SY, SC):
                        q[k].append(("w", "lx", 16))
                    if lo < nt:
                        send(wc(h, HELP[i]), "xs", lo, "xs", lo, nt - lo, "hx")
                else:
                    for k in (G, SY, SC):
                        q[k].append(("W", "hx"))
                o = 0
                outs = []
                for (lnd, lcol, toks, sem) in msgs.get(me, []):
                    for (k0, t0, m) in _runs(toks):
                        cp("pk", o + k0, "xs", t0, m, "ph")
                    outs.append((lnd, "ld", lcol, "pk", o, len(toks), sem))
                    o += len(toks)
                near = []
                for j in range(4):
                    lst = [(t, yc) for t in (range(0, sl[r]) if c < 4 else range(sl[r], nt))
                           for (e, yc) in dest[r][t] if e == 4 * h + j]
                    for (k0, t0, m) in _runs([t for t, _ in lst]):
                        if j == c:
                            cp("yi", lst[0][1] + k0, "xs", t0, m, "lh")
                        else:
                            cp("pk", o + k0, "xs", t0, m, "lh")
                    if lst and j != c:
                        near.append((wc(h, j), "yi", lst[0][1], "pk", o, len(lst), "arr"))
                        o += len(lst)
                size["pk"] = max(size["pk"], o)
                done("ph")
                for a in outs:
                    send(*a)
                done("lh")
                for a in near:
                    send(*a)
            for rel in ("sw", "cb"):
                if rel in fwds.get(me, {}):
                    far, o2, o1, m = fwds[me][rel]
                    q[G].append(("W", SEMS[rel][0]))
                    send(far, "ld", o2, "ld", o1, m, "dg")
            o = 0
            for rel in ("sw", "cb", "dg"):
                if rel not in units.get(me, {}):
                    continue
                s, p = units[me][rel]
                for k in (G, SY, SC):
                    for sem in sorted(set(SEMS[rel][:2])):
                        q[k].append(("W", sem))
                outs = []
                for j in range(4):
                    lst = [(col[(me, s, t)], yc) for t in (range(0, cut) if p == 0 else range(cut, nt))
                           for (e, yc) in dest[s][t] if e == 4 * h + j]
                    for (k0, c0, m) in _runs([a for a, _ in lst]):
                        if j == c:
                            cp("yi", lst[0][1] + k0, "ld", c0, m, SEMS[rel][2])
                        else:
                            cp("gp", o + k0, "ld", c0, m, SEMS[rel][2])
                    if lst and j != c:
                        outs.append((wc(h, j), "yi", lst[0][1], "gp", o, len(lst), "arr"))
                        o += len(lst)
                done(SEMS[rel][2])
                for a in outs:
                    send(*a)
            size["gp"] = max(size["gp"], o)
            if c < 4:
                q[G].append(("W", "arr"))
                q[G].append(("sty", cnt[4 * h + c], "st"))
                q[G].append(("w", "st", 16))
            q[G].append(("W", "sent"))
    for me in prog:
        prog[me] = [[(("w", op[1], total[(me, op[1])]) if op[0] == "W" else op)
                     for op in ql if op[0] != "W" or (me, op[1]) in total] for ql in prog[me]]
    return prog, size


def _plan(tables, cores):
    route, cap, nt = tables["ROUTE"], tables["CAP"], tables["T"]
    n = len(route)
    chip0 = [cores[4 * h] - cores[4 * h] % 8 for h in range(4)]

    def wc(h, c):
        return chip0[h] + c

    fill = [0] * n
    dest = [[None] * nt for _ in range(n)]
    for r in range(n):
        for t in range(nt):
            dest[r][t] = [(e, fill[e]) for e in route[r][t] if fill[e] < cap]
            for e in route[r][t]:
                fill[e] += 1
    cnt = [min(f, cap) for f in fill]
    sets, via = _ways(dest, n, nt)
    edge = {}
    for r in range(n):
        for d in (1, 3):
            on = [2 in sets[r][t] and via[r][t] == d for t in range(nt)]
            edge[(r, d)] = ([t for t in range(nt) if d in sets[r][t] and not on[t]], [t for t in range(nt) if on[t]])
    cut = nt * CUT // 16
    thr = _thresholds(edge, cut, nt)
    prog, _ = _emit(dest, cnt, edge, thr, cut, [nt] * n, nt, wc)
    sl = []
    for r in range(n):
        h, i = r // 4, r % 4
        a, b = [sum(1 for ql in prog[wc(h, c)] for op in ql if op[0] == "cp" and op[6] != "lh") for c in (i, HELP[i])]
        here = [set(e for e, _ in dest[r][t] if e // 4 == h) for t in range(nt)] + [set()]
        start = [len(here[t] - here[t - 1]) for t in range(nt)]
        best = None
        for s in range(nt, -1, -1):
            w = max(a + sum(start[:s]), b + sum(start[s:]) + len(here[s] & here[s - 1]))
            if best is None or w < best[0]:
                best = (w, s)
        sl.append(best[1])
    prog, size = _emit(dest, cnt, edge, thr, cut, sl, nt, wc)
    for k, v in size.items():
        assert v <= SCRATCH[k][1][1], (k, v)
    return prog, size


def rank_program(g, core, T, topo):
    if "plan" not in _CACHE:
        _CACHE["plan"] = _plan(T.tables, T.cores)[0]
    queues = _CACHE["plan"].get(core)
    if queues is None:
        return
    S = T.sem
    for eng, ql in zip((g, g.sync, g.scalar), queues):
        for op in ql:
            if op[0] == "cp":
                _, dst, dc, src, sc, m, sem = op
                eng.dma_start(T[dst][:, dc:dc + m], T[src][:, sc:sc + m]).then_inc(S[sem], 16)
            elif op[0] == "w":
                eng.wait_ge(S[op[1]], op[2])
            elif op[0] == "rd":
                _, to, dst, dc, src, sc, m, sem = op
                rid, pid = topo.addr(to, core)
                eng.remote_dma(T[dst][:, dc:dc + m], T[src][:, sc:sc + m], S[sem], S.sent, pid, rid,
                               topo.mask(core, to))
            elif op[0] == "ldx":
                eng.dma_start(T.xs[:], T.x[:]).then_inc(S[op[1]], 16)
            elif op[0] == "sty":
                eng.dma_start(T.y[:, 0:op[1]], T.yi[:, 0:op[1]]).then_inc(S[op[2]], 16)
